import numpy as np
import ml_dtypes


def mxq(x, axis, fmt="e4m3"):
    dtype, down = {"e4m3": (ml_dtypes.float8_e4m3fn, 7), "e5m2": (ml_dtypes.float8_e5m2, 14)}[fmt]
    v = np.moveaxis(np.asarray(x, np.float32).astype(ml_dtypes.bfloat16).astype(np.float64), axis, -1)
    blocks = v.reshape(v.shape[:-1] + (-1, 32))
    amax = np.abs(blocks).max(-1, keepdims=True)
    byte = np.maximum(np.where(amax > 0, np.frexp(amax)[1] - 1 + 127, 0) - down, 1)
    scale = np.exp2(byte - 127.0)
    codes = (blocks / scale).astype(np.float32).astype(dtype).astype(np.float64)
    return np.moveaxis((codes * scale).reshape(v.shape), -1, axis)


WIDE = False


def mx_kscale(k):
    if not WIDE:
        return np.ones(k)
    levels = np.array([10, -10, 5, -5, 0])
    if k % 512:
        return np.exp2(np.random.permutation(np.resize(levels, k // 32))).repeat(32)
    a = np.empty((k // 512, 16))
    for p in range(k // 512):
        a[p, :8] = np.random.permutation(np.resize(levels, 8))
        for g in range(8):
            far = levels[np.abs(levels - a[p, g]) >= 10]
            a[p, g + 8] = far[np.random.randint(len(far))]
    return np.exp2(a.ravel()).repeat(32)


def f64(x):
    return np.asarray(x).astype(np.float64)


def striped(idx):
    return np.tile(idx.reshape(-1, 16).T, (8, 1)).astype(np.uint16)


def unstriped(offs):
    return offs[:16].T.reshape(-1).astype(np.int64)


E2M1 = np.array([0.0, 0.5, 1.0, 1.5, 2.0, 3.0, 4.0, 6.0, -0.0, -0.5, -1.0, -1.5, -2.0, -3.0, -4.0, -6.0])


def pack_fp4(w):
    k, n = w.shape
    w = f64(np.asarray(w, np.float32).astype(ml_dtypes.bfloat16)).reshape(k // 32, 32, n)
    amax = np.abs(w).max(1)
    mant, ex = np.frexp(amax / 6.0)
    byte = np.clip(np.where(amax > 0, np.where(mant > 0.5, ex, ex - 1) + 127, 1), 1, 254)
    scaled = (w * np.exp2(127.0 - byte)[:, None, :]).reshape(k, n).astype(np.float32)
    c = np.ascontiguousarray(scaled.reshape(k // 512, 128, 4, n).transpose(0, 1, 3, 2)).astype(ml_dtypes.float4_e2m1fn).view(np.uint8) & 0xF
    words = (c[..., 0::2] | (c[..., 1::2] << 4)).reshape(k // 512, 128, 2 * n)
    return np.ascontiguousarray(words), np.ascontiguousarray(byte.astype(np.uint8).reshape(k // 512, 16, n))


def unpack_fp4(words, scales):
    g, _, n = scales.shape
    words = np.ascontiguousarray(words).reshape(g, 128, n, 2)
    nib = np.empty((g, 128, n, 4), np.uint8)
    nib[..., 0::2] = words & 0xF
    nib[..., 1::2] = words >> 4
    vals = E2M1[nib] * np.repeat(np.exp2(scales.astype(np.float64) - 127.0), 8, axis=1)[..., None]
    return vals.transpose(0, 1, 3, 2).reshape(g * 512, n)


K, T, S, D, V, N = 1024, 2048, 512, 2, 256, 256
P = 2 ** 7


def setup_inputs():
    n = np.random.standard_normal
    s = mx_kscale(K)[:, None]
    packed_xT = pack_fp4(n((K, T)) * s)
    return {
        "x_words": packed_xT[0],
        "x_scales": packed_xT[1],
        "w1": (n((K, N)) / np.sqrt(K) / s).astype(np.float32),
        "gate": (np.tile(np.random.uniform(0.2, 1.0, (D, 1, V)) / np.sqrt(D), (1, P, 1))).astype(np.float32),
        "offs": striped(np.random.permutation(T)[:S]),
        "cen": striped(np.random.permutation(S)[:V]),
        "pos1": striped(np.random.permutation(S)[:V]),
        "pos2": striped(np.random.permutation(S)[:V]),
    }


def reference(x_words, x_scales, w1, gate, offs, cen, pos1, pos2):
    xq = unpack_fp4(x_words, x_scales)[:, unstriped(offs)]
    y = mxq(f64(w1), 0, "e4m3").T @ xq
    yc = y[:, unstriped(cen)]
    return yc + (y[:, unstriped(pos1)] - yc) * f64(gate)[0, :1] + (y[:, unstriped(pos2)] - yc) * f64(gate)[1, :1]

@@ -1,0 +1,119 @@
+from contextlib import ExitStack
+
+import concourse.mybir as mybir
+
+K, T, S, V, N = 1024, 2048, 512, 256, 256
+P = 128
+FLOPS = 2 * K * N * S
+
+F32 = mybir.dt.float32
+BF16 = mybir.dt.bfloat16
+I32 = mybir.dt.int32
+U32 = mybir.dt.uint32
+U16 = mybir.dt.uint16
+U8 = mybir.dt.uint8
+FP8X4 = mybir.dt.float8_e4m3fn_x4
+FP4X4 = mybir.dt.float4_e2m1fn_x4
+ALU = mybir.AluOpType
+
+
+def tile_picked_grand_none_p_kernel(tc, x_words, x_scales, w1, gate, offs, cen, pos1, pos2, out):
+    nc = tc.nc
+    with ExitStack() as ctx:
+        keep = ctx.enter_context(tc.tile_pool(name="keep", bufs=1))
+        psum = ctx.enter_context(tc.psum_pool(name="psum", bufs=1))
+
+        offs_t = keep.tile([P, S // 16], U16, name="offs_t")
+        nc.sync.dma_start(offs_t[:], offs)
+
+        table_words = [keep.tile([P, T], U16, name="table_words%d" % z, align_bytes=64) for z in range(2)]
+        table_scales = keep.tile([P, 2 * T], U8, name="table_scales", align_bytes=64)
+        nc.vector.memset(table_scales[:].bitcast(I32), 0)
+        nc.sync.dma_start(table_words[0][:].bitcast(I32), x_words[0].bitcast(I32))
+        for q in range(4):
+            nc.sync.dma_start(
+                table_scales[32 * q : 32 * q + 4, :].bitcast(I32).rearrange("r (z c) -> r z c", z=2),
+                x_scales[:, 4 * q : 4 * q + 4, :].bitcast(I32).rearrange("z r c -> r z c"),
+            )
+        nc.sync.dma_start(table_words[1][:].bitcast(I32), x_words[1].bitcast(I32))
+
+        w_raw = {}
+        for b in range(2):
+            for z in range(2):
+                w_raw[b, z] = keep.tile([P, 4, P], F32, name="w_raw%d%d" % (b, z))
+                nc.sync.dma_start(
+                    w_raw[b, z][:],
+                    w1[512 * z : 512 * (z + 1), P * b : P * (b + 1)].rearrange("(p j) m -> p j m", j=4),
+                )
+        gates = keep.tile([P, 2, V], F32, name="gates")
+        nc.sync.dma_start(gates[:], gate.rearrange("d p v -> p d v"))
+        lists = []
+        for name, src in (("cen_t", cen), ("pos1_t", pos1), ("pos2_t", pos2)):
+            t = keep.tile([P, V // 16], U16, name=name)
+            nc.sync.dma_start(t[:], src)
+            lists.append(t)
+
+        picked_words = [keep.tile([P, S], U16, name="picked_words%d" % z, align_bytes=64) for z in range(2)]
+        picked_scales = [keep.tile([P, S], U8, name="picked_scales%d" % z, align_bytes=64) for z in range(2)]
+        nc.vector.tensor_copy(picked_words[0][:], table_words[0][:].indirect(offs_t[:]))
+        for z in range(2):
+            nc.vector.tensor_copy(picked_scales[z][:], table_scales[:, T * z : T * (z + 1)].indirect(offs_t[:]))
+        nc.vector.tensor_copy(picked_words[1][:], table_words[1][:].indirect(offs_t[:]))
+
+        w_codes, w_scales = {}, {}
+        for b in range(2):
+            for z in range(2):
+                grouped = keep.tile([P, P, 4], BF16, name="grouped%d%d" % (b, z), align_bytes=64)
+                nc.scalar.copy(
+                    grouped[:].rearrange("p (c i) t -> p c t i", i=4),
+                    w_raw[b, z][:].rearrange("p t (c i) -> p c t i", i=4),
+                )
+                w_codes[b, z] = keep.tile([P, P], U32, name="w_codes%d%d" % (b, z), align_bytes=64)
+                w_scales[b, z] = keep.tile([P, P], U8, name="w_scales%d%d" % (b, z), align_bytes=64)
+                nc.vector.quantize_mx(
+                    out=w_codes[b, z][:].bitcast(FP8X4),
+                    scales=w_scales[b, z][:],
+                    in_=grouped[:].rearrange("p c t -> p (c t)"),
+                )
+
+        minus_stay = keep.tile([P, V], F32, name="minus_stay")
+        nc.vector.scalar_tensor_tensor(minus_stay[:], gates[:, 0, :], 1.0, gates[:, 1, :], ALU.subtract, ALU.add)
+
+        def product(acc, b, z, cols):
+            nc.tensor.matmul_mx(
+                out=acc,
+                lhsT=w_codes[b, z][:].bitcast(FP8X4),
+                lhsT_scale=w_scales[b, z][:],
+                rhs=picked_words[z][:, cols].bitcast(FP4X4),
+                rhs_scale=picked_scales[z][:, cols],
+                start=(z == 0),
+                stop=(z == 1),
+            )
+
+        y = [keep.tile([P, S], F32, name="y%d" % b) for b in range(2)]
+        quarter = [psum.tile([P, P], F32, name="quarter%d" % g) for g in range(4)]
+        for z in range(2):
+            for g in range(4):
+                product(quarter[g][:], 0, z, slice(P * g, P * (g + 1)))
+        for g in range(4):
+            if g % 2 == 0:
+                nc.scalar.copy(y[0][:, P * g : P * (g + 1)], quarter[g][:])
+            else:
+                nc.vector.tensor_copy(y[0][:, P * g : P * (g + 1)], quarter[g][:])
+        whole = psum.tile([P, S], F32, name="whole")
+        for z in range(2):
+            product(whole[:], 1, z, slice(0, S))
+        nc.scalar.copy(y[1][:], whole[:])
+
+        for b in range(2):
+            t1 = keep.tile([P, V], F32, name="t1_%d" % b)
+            t2 = keep.tile([P, V], F32, name="t2_%d" % b)
+            t3 = keep.tile([P, V], F32, name="t3_%d" % b)
+            s12 = keep.tile([P, V], F32, name="s12_%d" % b)
+            res = keep.tile([P, V], F32, name="res_%d" % b)
+            nc.vector.tensor_tensor(t1[:], y[b][:].indirect(lists[1][:]), gates[:, 0, :], ALU.mult)
+            nc.vector.tensor_tensor(t2[:], y[b][:].indirect(lists[2][:]), gates[:, 1, :], ALU.mult)
+            nc.vector.tensor_tensor(t3[:], y[b][:].indirect(lists[0][:]), minus_stay[:], ALU.mult)
+            nc.vector.tensor_tensor(s12[:], t1[:], t2[:], ALU.add)
+            nc.vector.tensor_tensor(res[:], s12[:], t3[:], ALU.subtract)
+            nc.sync.dma_start(out[P * b : P * (b + 1), :], res[:])

@@ -1,6 +1,7 @@
 from contextlib import ExitStack
 
 import concourse.mybir as mybir
+from concourse.masks import make_identity
 
 K, T, S, V, N = 1024, 2048, 512, 256, 256
 P = 128
@@ -9,8 +10,8 @@ FLOPS = 2 * K * N * S
 F32 = mybir.dt.float32
 BF16 = mybir.dt.bfloat16
 I32 = mybir.dt.int32
-U32 = mybir.dt.uint32
 U16 = mybir.dt.uint16
+U32 = mybir.dt.uint32
 U8 = mybir.dt.uint8
 FP8X4 = mybir.dt.float8_e4m3fn_x4
 FP4X4 = mybir.dt.float4_e2m1fn_x4
@@ -23,97 +24,138 @@ def tile_picked_grand_none_p_kernel(tc, x_words, x_scales, w1, gate, offs, cen, 
         keep = ctx.enter_context(tc.tile_pool(name="keep", bufs=1))
         psum = ctx.enter_context(tc.psum_pool(name="psum", bufs=1))
 
-        offs_t = keep.tile([P, S // 16], U16, name="offs_t")
-        nc.sync.dma_start(offs_t[:], offs)
+        def load_list(name, src):
+            tile = keep.tile([P, src.shape[1]], U16, name=name)
+            nc.sync.dma_start(tile[:], src)
+            return tile
 
-        table_words = [keep.tile([P, T], U16, name="table_words%d" % z, align_bytes=64) for z in range(2)]
-        table_scales = keep.tile([P, 2 * T], U8, name="table_scales", align_bytes=64)
+        table_words = [keep.tile([P, T], U16, name="table_words%d" % z, tag="first%d" % z, align_bytes=64) for z in range(2)]
+        table_scales = keep.tile([P, T], U8, name="table_scales", align_bytes=64)
         nc.vector.memset(table_scales[:].bitcast(I32), 0)
+        moved_scales = keep.tile([P, S], U8, name="moved_scales", align_bytes=64)
+        nc.vector.memset(moved_scales[:].bitcast(I32), 0)
+        ident = keep.tile([P, P], F32, name="ident")
+        make_identity(nc, ident[:])
+
         nc.sync.dma_start(table_words[0][:].bitcast(I32), x_words[0].bitcast(I32))
-        for q in range(4):
-            nc.sync.dma_start(
-                table_scales[32 * q : 32 * q + 4, :].bitcast(I32).rearrange("r (z c) -> r z c", z=2),
-                x_scales[:, 4 * q : 4 * q + 4, :].bitcast(I32).rearrange("z r c -> r z c"),
-            )
+        offs_t = load_list("offs_t", offs)
+        scale_rows = x_scales.bitcast(I32).rearrange("z (q r) c -> r q z c", r=4)
+        for r in range(4):
+            nc.sync.dma_start(table_scales[r:P:16, :].bitcast(I32), scale_rows[r])
         nc.sync.dma_start(table_words[1][:].bitcast(I32), x_words[1].bitcast(I32))
 
         w_raw = {}
-        for b in range(2):
-            for z in range(2):
-                w_raw[b, z] = keep.tile([P, 4, P], F32, name="w_raw%d%d" % (b, z))
-                nc.sync.dma_start(
-                    w_raw[b, z][:],
-                    w1[512 * z : 512 * (z + 1), P * b : P * (b + 1)].rearrange("(p j) m -> p j m", j=4),
-                )
+
+        def load_w(b, z):
+            w_raw[b, z] = keep.tile([P, 4, P], F32, name="w_raw%d%d" % (b, z))
+            nc.sync.dma_start(
+                w_raw[b, z][:],
+                w1[512 * z : 512 * (z + 1), P * b : P * (b + 1)].rearrange("(p j) m -> p j m", j=4),
+            )
+
+        load_w(0, 0)
+        pos1_t = load_list("pos1_t", pos1)
+        pos2_t = load_list("pos2_t", pos2)
+        cen_t = load_list("cen_t", cen)
+        load_w(0, 1)
+        load_w(1, 0)
+        load_w(1, 1)
         gates = keep.tile([P, 2, V], F32, name="gates")
         nc.sync.dma_start(gates[:], gate.rearrange("d p v -> p d v"))
-        lists = []
-        for name, src in (("cen_t", cen), ("pos1_t", pos1), ("pos2_t", pos2)):
-            t = keep.tile([P, V // 16], U16, name=name)
-            nc.sync.dma_start(t[:], src)
-            lists.append(t)
 
-        picked_words = [keep.tile([P, S], U16, name="picked_words%d" % z, align_bytes=64) for z in range(2)]
-        picked_scales = [keep.tile([P, S], U8, name="picked_scales%d" % z, align_bytes=64) for z in range(2)]
-        nc.vector.tensor_copy(picked_words[0][:], table_words[0][:].indirect(offs_t[:]))
-        for z in range(2):
-            nc.vector.tensor_copy(picked_scales[z][:], table_scales[:, T * z : T * (z + 1)].indirect(offs_t[:]))
-        nc.vector.tensor_copy(picked_words[1][:], table_words[1][:].indirect(offs_t[:]))
+        picked_words0 = keep.tile([P, S], U16, name="picked_words0", align_bytes=64)
+        nc.vector.tensor_copy(picked_words0[:], table_words[0][:].indirect(offs_t[:]))
+        picked_scales = keep.tile([P, S], U8, name="picked_scales", tag="first0", align_bytes=64)
+        nc.vector.tensor_copy(picked_scales[:], table_scales[:].indirect(offs_t[:]))
+        for q in range(4):
+            nc.sync.dma_start(moved_scales[32 * q : 32 * q + 4, :].bitcast(I32), picked_scales[32 * q + 16 : 32 * q + 20, :].bitcast(I32))
+        x_planes = [picked_scales, moved_scales]
 
-        w_codes, w_scales = {}, {}
-        for b in range(2):
-            for z in range(2):
-                grouped = keep.tile([P, P, 4], BF16, name="grouped%d%d" % (b, z), align_bytes=64)
-                nc.scalar.copy(
-                    grouped[:].rearrange("p (c i) t -> p c t i", i=4),
-                    w_raw[b, z][:].rearrange("p t (c i) -> p c t i", i=4),
-                )
-                w_codes[b, z] = keep.tile([P, P], U32, name="w_codes%d%d" % (b, z), align_bytes=64)
-                w_scales[b, z] = keep.tile([P, P], U8, name="w_scales%d%d" % (b, z), align_bytes=64)
-                nc.vector.quantize_mx(
-                    out=w_codes[b, z][:].bitcast(FP8X4),
-                    scales=w_scales[b, z][:],
-                    in_=grouped[:].rearrange("p c t -> p (c t)"),
-                )
+        def quantise(b, z):
+            grouped = keep.tile([P, P, 4], BF16, name="grouped%d%d" % (b, z), tag="grouped%d%d" % (b, z), align_bytes=64)
+            nc.scalar.copy(
+                grouped[:].rearrange("p (c i) t -> p c t i", i=4),
+                w_raw[b, z][:].rearrange("p t (c i) -> p c t i", i=4),
+            )
+            codes = keep.tile([P, P], U32, name="w_codes%d%d" % (b, z), align_bytes=64)
+            plane = keep.tile([P, P], U8, name="w_scales%d%d" % (b, z), align_bytes=64)
+            nc.vector.quantize_mx(out=codes[:].bitcast(FP8X4), scales=plane[:], in_=grouped[:].rearrange("p c t -> p (c t)"))
+            return codes, plane
 
-        minus_stay = keep.tile([P, V], F32, name="minus_stay")
-        nc.vector.scalar_tensor_tensor(minus_stay[:], gates[:, 0, :], 1.0, gates[:, 1, :], ALU.subtract, ALU.add)
-
-        def product(acc, b, z, cols):
+        def product(acc, weights, z, words, cols, start, stop):
+            codes, plane = weights
             nc.tensor.matmul_mx(
                 out=acc,
-                lhsT=w_codes[b, z][:].bitcast(FP8X4),
-                lhsT_scale=w_scales[b, z][:],
-                rhs=picked_words[z][:, cols].bitcast(FP4X4),
-                rhs_scale=picked_scales[z][:, cols],
-                start=(z == 0),
-                stop=(z == 1),
+                lhsT=codes[:].bitcast(FP8X4),
+                lhsT_scale=plane[:],
+                rhs=words.bitcast(FP4X4),
+                rhs_scale=x_planes[z][:, cols],
+                start=start,
+                stop=stop,
             )
 
         y = [keep.tile([P, S], F32, name="y%d" % b) for b in range(2)]
-        quarter = [psum.tile([P, P], F32, name="quarter%d" % g) for g in range(4)]
+        weights = {(0, z): quantise(0, z) for z in range(2)}
+        half = S // 2
+        picked_half = []
+        for u in range(2):
+            tile = keep.tile([P, half], U16, name="picked_words1%d" % u, tag="grouped0%d" % u, align_bytes=64)
+            nc.vector.tensor_copy(tile[:], table_words[1][:].indirect(offs_t[:, 16 * u : 16 * (u + 1)]))
+            picked_half.append(tile)
         for z in range(2):
-            for g in range(4):
-                product(quarter[g][:], 0, z, slice(P * g, P * (g + 1)))
-        for g in range(4):
-            if g % 2 == 0:
-                nc.scalar.copy(y[0][:, P * g : P * (g + 1)], quarter[g][:])
-            else:
-                nc.vector.tensor_copy(y[0][:, P * g : P * (g + 1)], quarter[g][:])
-        whole = psum.tile([P, S], F32, name="whole")
-        for z in range(2):
-            product(whole[:], 1, z, slice(0, S))
-        nc.scalar.copy(y[1][:], whole[:])
+            weights[1, z] = quantise(1, z)
+        rest = keep.tile([P, V], F32, name="rest")
+        nc.vector.tensor_scalar(rest[:], gates[:, 0, :], -1.0, 1.0, ALU.mult, ALU.add)
+        stay = keep.tile([P, V], F32, name="stay")
+        nc.vector.tensor_tensor(stay[:], rest[:], gates[:, 1, :], ALU.subtract)
 
-        for b in range(2):
-            t1 = keep.tile([P, V], F32, name="t1_%d" % b)
-            t2 = keep.tile([P, V], F32, name="t2_%d" % b)
-            t3 = keep.tile([P, V], F32, name="t3_%d" % b)
-            s12 = keep.tile([P, V], F32, name="s12_%d" % b)
-            res = keep.tile([P, V], F32, name="res_%d" % b)
-            nc.vector.tensor_tensor(t1[:], y[b][:].indirect(lists[1][:]), gates[:, 0, :], ALU.mult)
-            nc.vector.tensor_tensor(t2[:], y[b][:].indirect(lists[2][:]), gates[:, 1, :], ALU.mult)
-            nc.vector.tensor_tensor(t3[:], y[b][:].indirect(lists[0][:]), minus_stay[:], ALU.mult)
-            nc.vector.tensor_tensor(s12[:], t1[:], t2[:], ALU.add)
-            nc.vector.tensor_tensor(res[:], s12[:], t3[:], ALU.subtract)
-            nc.sync.dma_start(out[P * b : P * (b + 1), :], res[:])
+        def project(b, pieces):
+            banks = [psum.tile([P, len(piece), P], F32, name="bank%d%d" % (b, i), tag=tag) for i, (piece, tag, copy) in enumerate(pieces)]
+            for z in range(2):
+                for bank, (piece, tag, copy) in zip(banks, pieces):
+                    for i, g in enumerate(piece):
+                        cols = slice(P * g, P * (g + 1))
+                        words = picked_words0[:, cols] if z == 0 else picked_half[g // 2][:, P * (g % 2) : P * (g % 2 + 1)]
+                        product(bank[:, i, :], weights[b, z], z, words, cols, z == 0 and i == 0, z == 1 and i == len(piece) - 1)
+                    if z == 1:
+                        copy(y[b][:, P * piece[0] : P * (piece[-1] + 1)], bank[:].rearrange("p g c -> p (g c)"))
+
+        project(0, [((0, 1), "a", nc.scalar.copy), ((2,), "b", nc.scalar.copy), ((3,), "c", nc.vector.tensor_copy)])
+        project(1, [((0, 1), "d", nc.scalar.copy), ((2, 3), "e", nc.scalar.copy)])
+
+        terms = [(pos1_t, gates[:, 0, :]), (pos2_t, gates[:, 1, :]), (cen_t, stay[:])]
+
+        def weighted(b, d):
+            places, factor = terms[d]
+            term = keep.tile([P, V], F32, name="term%d%d" % (b, d))
+            nc.vector.tensor_tensor(term[:], y[b][:].indirect(places[:]), factor, ALU.mult)
+            return term
+
+        turned = psum.tile([P, 2, P], F32, name="turned")
+
+        def add_turned(d):
+            term = weighted(0, d)
+            for h in range(2):
+                nc.tensor.matmul(
+                    turned[:, h, :], term[:, P * h : P * (h + 1)], ident[:],
+                    start=(d == 0 and h == 0), stop=(d == 2 and h == 1), is_transpose=True,
+                )
+
+        for d in range(3):
+            add_turned(d)
+
+        turned_sum = keep.tile([P, 2, P], F32, name="turned_sum")
+        nc.scalar.copy(turned_sum[:], turned[:])
+        back = psum.tile([P, 2, P], F32, name="back")
+        for h in range(2):
+            nc.tensor.transpose(back[:, h, :], turned_sum[:, h, :], ident[:])
+        res0 = keep.tile([P, V], F32, name="res0")
+        nc.scalar.copy(res0[:], back[:].rearrange("p h v -> p (h v)"))
+        nc.sync.dma_start(out[0:P, :], res0[:])
+
+        t = [weighted(1, d) for d in range(3)]
+        pair = keep.tile([P, V], F32, name="pair")
+        res1 = keep.tile([P, V], F32, name="res1")
+        nc.vector.tensor_tensor(pair[:], t[0][:], t[1][:], ALU.add)
+        nc.vector.tensor_tensor(res1[:], pair[:], t[2][:], ALU.add)
+        nc.sync.dma_start(out[P : 2 * P, :], res1[:])

@@ -44,22 +44,16 @@ def tile_picked_grand_none_p_kernel(tc, x_words, x_scales, w1, gate, offs, cen, 
             nc.sync.dma_start(table_scales[r:P:16, :].bitcast(I32), scale_rows[r])
         nc.sync.dma_start(table_words[1][:].bitcast(I32), x_words[1].bitcast(I32))
 
-        w_raw = {}
+        w_raw = [keep.tile([P, 4, N], F32, name="w_raw%d" % z) for z in range(2)]
 
-        def load_w(b, z):
-            w_raw[b, z] = keep.tile([P, 4, P], F32, name="w_raw%d%d" % (b, z))
-            nc.sync.dma_start(
-                w_raw[b, z][:],
-                w1[512 * z : 512 * (z + 1), P * b : P * (b + 1)].rearrange("(p j) m -> p j m", j=4),
-            )
+        def load_w(z):
+            nc.sync.dma_start(w_raw[z][:], w1[512 * z : 512 * (z + 1), :].rearrange("(p j) m -> p j m", j=4))
 
-        load_w(0, 0)
+        load_w(0)
         pos1_t = load_list("pos1_t", pos1)
         pos2_t = load_list("pos2_t", pos2)
         cen_t = load_list("cen_t", cen)
-        load_w(0, 1)
-        load_w(1, 0)
-        load_w(1, 1)
+        load_w(1)
         gates = keep.tile([P, 2, V], F32, name="gates")
         nc.sync.dma_start(gates[:], gate.rearrange("d p v -> p d v"))
 
@@ -67,15 +61,18 @@ def tile_picked_grand_none_p_kernel(tc, x_words, x_scales, w1, gate, offs, cen, 
         nc.vector.tensor_copy(picked_words0[:], table_words[0][:].indirect(offs_t[:]))
         picked_scales = keep.tile([P, S], U8, name="picked_scales", tag="first0", align_bytes=64)
         nc.vector.tensor_copy(picked_scales[:], table_scales[:].indirect(offs_t[:]))
-        for q in range(4):
-            nc.sync.dma_start(moved_scales[32 * q : 32 * q + 4, :].bitcast(I32), picked_scales[32 * q + 16 : 32 * q + 20, :].bitcast(I32))
+        for first, count in ((0, 64), (64, 4), (96, 4)):
+            nc.sync.dma_start(moved_scales[first : first + count, :].bitcast(I32), picked_scales[first + 16 : first + 16 + count, :].bitcast(I32))
         x_planes = [picked_scales, moved_scales]
+        picked_words1 = keep.tile([P, S], U16, name="picked_words1", align_bytes=64)
+        nc.vector.tensor_copy(picked_words1[:], table_words[1][:].indirect(offs_t[:]))
+        x_codes = [picked_words0, picked_words1]
 
         def quantise(b, z):
             grouped = keep.tile([P, P, 4], BF16, name="grouped%d%d" % (b, z), tag="grouped%d%d" % (b, z), align_bytes=64)
             nc.scalar.copy(
                 grouped[:].rearrange("p (c i) t -> p c t i", i=4),
-                w_raw[b, z][:].rearrange("p t (c i) -> p c t i", i=4),
+                w_raw[z][:, :, P * b : P * (b + 1)].rearrange("p t (c i) -> p c t i", i=4),
             )
             codes = keep.tile([P, P], U32, name="w_codes%d%d" % (b, z), align_bytes=64)
             plane = keep.tile([P, P], U8, name="w_scales%d%d" % (b, z), align_bytes=64)
@@ -95,15 +92,7 @@ def tile_picked_grand_none_p_kernel(tc, x_words, x_scales, w1, gate, offs, cen, 
             )
 
         y = [keep.tile([P, S], F32, name="y%d" % b) for b in range(2)]
-        weights = {(0, z): quantise(0, z) for z in range(2)}
-        half = S // 2
-        picked_half = []
-        for u in range(2):
-            tile = keep.tile([P, half], U16, name="picked_words1%d" % u, tag="grouped0%d" % u, align_bytes=64)
-            nc.vector.tensor_copy(tile[:], table_words[1][:].indirect(offs_t[:, 16 * u : 16 * (u + 1)]))
-            picked_half.append(tile)
-        for z in range(2):
-            weights[1, z] = quantise(1, z)
+        weights = {(b, z): quantise(b, z) for b in range(2) for z in range(2)}
         rest = keep.tile([P, V], F32, name="rest")
         nc.vector.tensor_scalar(rest[:], gates[:, 0, :], -1.0, 1.0, ALU.mult, ALU.add)
         stay = keep.tile([P, V], F32, name="stay")
@@ -115,12 +104,12 @@ def tile_picked_grand_none_p_kernel(tc, x_words, x_scales, w1, gate, offs, cen, 
                 for bank, (piece, tag, copy) in zip(banks, pieces):
                     for i, g in enumerate(piece):
                         cols = slice(P * g, P * (g + 1))
-                        words = picked_words0[:, cols] if z == 0 else picked_half[g // 2][:, P * (g % 2) : P * (g % 2 + 1)]
+                        words = x_codes[z][:, cols]
                         product(bank[:, i, :], weights[b, z], z, words, cols, z == 0 and i == 0, z == 1 and i == len(piece) - 1)
                     if z == 1:
                         copy(y[b][:, P * piece[0] : P * (piece[-1] + 1)], bank[:].rearrange("p g c -> p (g c)"))
 
-        project(0, [((0, 1), "a", nc.scalar.copy), ((2,), "b", nc.scalar.copy), ((3,), "c", nc.vector.tensor_copy)])
+        project(0, [((0,), "a", nc.scalar.copy), ((1,), "b", nc.vector.tensor_copy), ((2,), "c", nc.scalar.copy), ((3,), "f", nc.vector.tensor_copy)])
         project(1, [((0, 1), "d", nc.scalar.copy), ((2, 3), "e", nc.scalar.copy)])
 
         terms = [(pos1_t, gates[:, 0, :]), (pos2_t, gates[:, 1, :]), (cen_t, stay[:])]

@@ -16,101 +16,152 @@ U8 = mybir.dt.uint8
 FP8X4 = mybir.dt.float8_e4m3fn_x4
 FP4X4 = mybir.dt.float4_e2m1fn_x4
 ALU = mybir.AluOpType
+COPY = mybir.ActivationFunctionType.Copy
 
 
 def tile_picked_grand_none_p_kernel(tc, x_words, x_scales, w1, gate, offs, cen, pos1, pos2, out):
     nc = tc.nc
     with ExitStack() as ctx:
         keep = ctx.enter_context(tc.tile_pool(name="keep", bufs=1))
+        reused = ctx.enter_context(tc.tile_pool(name="reused", bufs=1))
         psum = ctx.enter_context(tc.psum_pool(name="psum", bufs=1))
+
+        at = {"table_scales": 0, "gate_cols": 2048}
+        at["picked_words0"] = at["table_scales"]
+        for i, name in enumerate(("grouped00", "grouped10", "grouped01", "grouped11")):
+            at[name] = at["gate_cols"] + 1024 * i
+        at["picked_words1"] = at["grouped00"]
+        at["w_codes10"] = at["grouped01"]
+        at["w_codes01"] = at["gate_cols"] + 4096
+        at["stay"] = at["w_codes01"]
+
+        def sbuf(name, shape, dtype):
+            if name in at:
+                return reused.tile(shape, dtype, name=name, offset=at[name], align_bytes=64)
+            return keep.tile(shape, dtype, name=name, align_bytes=64)
 
         def load_list(name, src):
             tile = keep.tile([P, src.shape[1]], U16, name=name)
             nc.sync.dma_start(tile[:], src)
             return tile
 
-        table_words = [keep.tile([P, T], U16, name="table_words%d" % z, tag="first%d" % z, align_bytes=64) for z in range(2)]
-        table_scales = keep.tile([P, T], U8, name="table_scales", align_bytes=64)
+        table_words = [sbuf("table_words%d" % z, [P, T], U16) for z in range(2)]
+        table_scales = sbuf("table_scales", [P, T], U8)
         nc.vector.memset(table_scales[:].bitcast(I32), 0)
-        moved_scales = keep.tile([P, S], U8, name="moved_scales", align_bytes=64)
-        nc.vector.memset(moved_scales[:].bitcast(I32), 0)
+        gate_rows = sbuf("gate_rows", [P, P], F32)
+        nc.gpsimd.memset(gate_rows[:], 0.0)
         ident = keep.tile([P, P], F32, name="ident")
         make_identity(nc, ident[:])
+        moved_scales = keep.tile([P, S], U8, name="moved_scales", align_bytes=64)
+        nc.gpsimd.memset(moved_scales[:].bitcast(I32), 0)
+        w_raw0 = sbuf("w_raw0", [P, 4, N], F32)
+        w_raw1 = [sbuf("w_raw1%d" % b, [P, 4, P], F32) for b in range(2)]
+        w_raw = {(b, 0): w_raw0[:, :, P * b : P * (b + 1)] for b in range(2)}
+        for b in range(2):
+            w_raw[b, 1] = w_raw1[b][:]
 
-        nc.sync.dma_start(table_words[0][:].bitcast(I32), x_words[0].bitcast(I32))
+        def load_words(z):
+            nc.sync.dma_start(table_words[z][:].bitcast(I32), x_words[z].bitcast(I32))
+
+        w_rows = w1.rearrange("(z p j) m -> z p j m", z=2, j=4)
+
         offs_t = load_list("offs_t", offs)
+        nc.sync.dma_start(w_raw0[:, 0:2, :], w_rows[0][:, 0:2, :])
+        nc.sync.dma_start(gate_rows[0:4, :], gate[:, 0, :].rearrange("d (h v) -> h d v", h=2))
         scale_rows = x_scales.bitcast(I32).rearrange("z (q r) c -> r q z c", r=4)
         for r in range(4):
-            nc.sync.dma_start(table_scales[r:P:16, :].bitcast(I32), scale_rows[r])
-        nc.sync.dma_start(table_words[1][:].bitcast(I32), x_words[1].bitcast(I32))
-
-        w_raw = [keep.tile([P, 4, N], F32, name="w_raw%d" % z) for z in range(2)]
-
-        def load_w(z):
-            nc.sync.dma_start(w_raw[z][:], w1[512 * z : 512 * (z + 1), :].rearrange("(p j) m -> p j m", j=4))
-
-        load_w(0)
+            (nc.sync if r < 2 else nc.scalar).dma_start(table_scales[r:P:16, :].bitcast(I32), scale_rows[r])
+        load_words(0)
+        nc.sync.dma_start(w_raw0[:, 2:4, :], w_rows[0][:, 2:4, :])
         pos1_t = load_list("pos1_t", pos1)
         pos2_t = load_list("pos2_t", pos2)
         cen_t = load_list("cen_t", cen)
-        load_w(1)
-        gates = keep.tile([P, 2, V], F32, name="gates")
-        nc.sync.dma_start(gates[:], gate.rearrange("d p v -> p d v"))
+        load_words(1)
+        for b in range(2):
+            nc.sync.dma_start(w_raw1[b][:], w_rows[1][:, :, P * b : P * (b + 1)])
 
-        picked_words0 = keep.tile([P, S], U16, name="picked_words0", align_bytes=64)
-        nc.vector.tensor_copy(picked_words0[:], table_words[0][:].indirect(offs_t[:]))
-        picked_scales = keep.tile([P, S], U8, name="picked_scales", tag="first0", align_bytes=64)
+        gate_cols_ps = psum.tile([P, P], F32, name="gate_cols_ps", tag="t0")
+        nc.tensor.transpose(gate_cols_ps[:], gate_rows[:], ident[:])
+        gate_cols = sbuf("gate_cols", [P, 1024], F32)
+        nc.scalar.copy(gate_cols[:, 0:4], gate_cols_ps[:, 0:4])
+        spread = psum.tile([P, 2, 2, P], F32, name="spread", tag="t1")
+        spread_sum = psum.tile([P, 2, P], F32, name="spread_sum", tag="t0")
+        for d in range(2):
+            for h in range(2):
+                nc.tensor.transpose(spread[:, d, h, :], gate_cols[:, 2 * h + d : 2 * h + d + 1].to_broadcast([P, P]), ident[:])
+        for d in range(2):
+            for h in range(2):
+                nc.tensor.matmul(
+                    spread_sum[:, h, :], gate_cols[:, 2 * h + d : 2 * h + d + 1].to_broadcast([P, P]), ident[:],
+                    start=(d == 0 and h == 0), stop=(d == 1 and h == 1), is_transpose=True,
+                )
+
+        gates = sbuf("gates", [P, 2, V], F32)
+        nc.scalar.copy(gates[:].rearrange("p d v -> p (d v)"), spread[:].rearrange("p d h v -> p (d h v)"))
+
+        picked_scales = keep.tile([P, S], U8, name="picked_scales", align_bytes=64)
         nc.vector.tensor_copy(picked_scales[:], table_scales[:].indirect(offs_t[:]))
-        for first, count in ((0, 64), (64, 4), (96, 4)):
-            nc.sync.dma_start(moved_scales[first : first + count, :].bitcast(I32), picked_scales[first + 16 : first + 16 + count, :].bitcast(I32))
+        picked_words = [sbuf("picked_words0", [P, S], U16)]
+        nc.vector.tensor_copy(picked_words[0][:], table_words[0][:].indirect(offs_t[:]))
+        for q in range(4):
+            nc.sync.dma_start(moved_scales[32 * q : 32 * q + 4, :].bitcast(I32), picked_scales[32 * q + 16 : 32 * q + 20, :].bitcast(I32))
         x_planes = [picked_scales, moved_scales]
-        picked_words1 = keep.tile([P, S], U16, name="picked_words1", align_bytes=64)
-        nc.vector.tensor_copy(picked_words1[:], table_words[1][:].indirect(offs_t[:]))
-        x_codes = [picked_words0, picked_words1]
 
-        def quantise(b, z):
-            grouped = keep.tile([P, P, 4], BF16, name="grouped%d%d" % (b, z), tag="grouped%d%d" % (b, z), align_bytes=64)
-            nc.scalar.copy(
+        def cast(b, z, copy):
+            grouped = sbuf("grouped%d%d" % (b, z), [P, P, 4], BF16)
+            copy(
                 grouped[:].rearrange("p (c i) t -> p c t i", i=4),
-                w_raw[z][:, :, P * b : P * (b + 1)].rearrange("p t (c i) -> p c t i", i=4),
+                w_raw[b, z].rearrange("p t (c i) -> p c t i", i=4),
             )
-            codes = keep.tile([P, P], U32, name="w_codes%d%d" % (b, z), align_bytes=64)
+            return grouped
+
+        def quantise(b, z, grouped):
+            codes = sbuf("w_codes%d%d" % (b, z), [P, P], U32)
             plane = keep.tile([P, P], U8, name="w_scales%d%d" % (b, z), align_bytes=64)
             nc.vector.quantize_mx(out=codes[:].bitcast(FP8X4), scales=plane[:], in_=grouped[:].rearrange("p c t -> p (c t)"))
             return codes, plane
 
-        def product(acc, weights, z, words, cols, start, stop):
-            codes, plane = weights
-            nc.tensor.matmul_mx(
-                out=acc,
-                lhsT=codes[:].bitcast(FP8X4),
-                lhsT_scale=plane[:],
-                rhs=words.bitcast(FP4X4),
-                rhs_scale=x_planes[z][:, cols],
-                start=start,
-                stop=stop,
-            )
+        weights = {}
+        weights[0, 0] = quantise(0, 0, cast(0, 0, nc.scalar.copy))
+        late = cast(1, 0, nc.scalar.copy)
+        picked_words.append(sbuf("picked_words1", [P, S], U16))
+        nc.vector.tensor_copy(picked_words[1][:], table_words[1][:].indirect(offs_t[:]))
+        weights[0, 1] = quantise(0, 1, cast(0, 1, nc.scalar.copy))
+        weights[1, 0] = quantise(1, 0, late)
+        weights[1, 1] = quantise(1, 1, cast(1, 1, nc.scalar.copy))
 
         y = [keep.tile([P, S], F32, name="y%d" % b) for b in range(2)]
-        weights = {(b, z): quantise(b, z) for b in range(2) for z in range(2)}
-        rest = keep.tile([P, V], F32, name="rest")
-        nc.vector.tensor_scalar(rest[:], gates[:, 0, :], -1.0, 1.0, ALU.mult, ALU.add)
-        stay = keep.tile([P, V], F32, name="stay")
-        nc.vector.tensor_tensor(stay[:], rest[:], gates[:, 1, :], ALU.subtract)
+        pieces = {
+            0: [((0,), nc.scalar.copy), ((1,), nc.vector.tensor_copy), ((2,), nc.scalar.copy), ((3,), nc.vector.tensor_copy)],
+            1: [((0, 1), nc.scalar.copy), ((2, 3), nc.scalar.copy)],
+        }
+        banks = {
+            b: [psum.tile([P, len(piece), P], F32, name="bank%d%d" % (b, i)) for i, (piece, copy) in enumerate(pieces[b])] for b in range(2)
+        }
 
-        def project(b, pieces):
-            banks = [psum.tile([P, len(piece), P], F32, name="bank%d%d" % (b, i), tag=tag) for i, (piece, tag, copy) in enumerate(pieces)]
-            for z in range(2):
-                for bank, (piece, tag, copy) in zip(banks, pieces):
-                    for i, g in enumerate(piece):
-                        cols = slice(P * g, P * (g + 1))
-                        words = x_codes[z][:, cols]
-                        product(bank[:, i, :], weights[b, z], z, words, cols, z == 0 and i == 0, z == 1 and i == len(piece) - 1)
-                    if z == 1:
-                        copy(y[b][:, P * piece[0] : P * (piece[-1] + 1)], bank[:].rearrange("p g c -> p (g c)"))
+        def project(b, z, first):
+            codes, plane = weights[b, z]
+            for bank, (piece, copy) in zip(banks[b], pieces[b]):
+                for i, g in enumerate(piece):
+                    cols = slice(P * g, P * (g + 1))
+                    nc.tensor.matmul_mx(
+                        out=bank[:, i, :],
+                        lhsT=codes[:].bitcast(FP8X4),
+                        lhsT_scale=plane[:],
+                        rhs=picked_words[z][:, cols].bitcast(FP4X4),
+                        rhs_scale=x_planes[z][:, cols],
+                        start=first and i == 0,
+                        stop=not first and i == len(piece) - 1,
+                    )
+                if not first:
+                    copy(y[b][:, P * piece[0] : P * (piece[-1] + 1)], bank[:].rearrange("p g c -> p (g c)"))
 
-        project(0, [((0,), "a", nc.scalar.copy), ((1,), "b", nc.vector.tensor_copy), ((2,), "c", nc.scalar.copy), ((3,), "f", nc.vector.tensor_copy)])
-        project(1, [((0, 1), "d", nc.scalar.copy), ((2, 3), "e", nc.scalar.copy)])
+        project(0, 0, True)
+        project(0, 1, False)
+        stay = sbuf("stay", [P, V], F32)
+        nc.scalar.activation(stay[:], spread_sum[:].rearrange("p h v -> p (h v)"), COPY, bias=1.0, scale=-1.0)
+        project(1, 1, True)
+        project(1, 0, False)
 
         terms = [(pos1_t, gates[:, 0, :]), (pos2_t, gates[:, 1, :]), (cen_t, stay[:])]
 
@@ -120,31 +171,35 @@ def tile_picked_grand_none_p_kernel(tc, x_words, x_scales, w1, gate, offs, cen, 
             nc.vector.tensor_tensor(term[:], y[b][:].indirect(places[:]), factor, ALU.mult)
             return term
 
-        turned = psum.tile([P, 2, P], F32, name="turned")
-
-        def add_turned(d):
+        turned = psum.tile([P, 2, P], F32, name="turned", tag="t0")
+        for d in range(3):
             term = weighted(0, d)
             for h in range(2):
                 nc.tensor.matmul(
                     turned[:, h, :], term[:, P * h : P * (h + 1)], ident[:],
                     start=(d == 0 and h == 0), stop=(d == 2 and h == 1), is_transpose=True,
                 )
-
-        for d in range(3):
-            add_turned(d)
-
         turned_sum = keep.tile([P, 2, P], F32, name="turned_sum")
         nc.scalar.copy(turned_sum[:], turned[:])
-        back = psum.tile([P, 2, P], F32, name="back")
+        back = psum.tile([P, 2, P], F32, name="back", tag="t1")
         for h in range(2):
             nc.tensor.transpose(back[:, h, :], turned_sum[:, h, :], ident[:])
         res0 = keep.tile([P, V], F32, name="res0")
         nc.scalar.copy(res0[:], back[:].rearrange("p h v -> p (h v)"))
         nc.sync.dma_start(out[0:P, :], res0[:])
 
-        t = [weighted(1, d) for d in range(3)]
+        t = [weighted(1, d) for d in range(2)]
         pair = keep.tile([P, V], F32, name="pair")
         res1 = keep.tile([P, V], F32, name="res1")
+        halves = [slice(0, V // 2), slice(V // 2, V)]
+        own = [keep.tile([P, V // 2], F32, name="own%d" % h) for h in range(2)]
+
+        def own_term(h):
+            nc.vector.tensor_tensor(own[h][:], y[1][:].indirect(cen_t[:, 8 * h : 8 * (h + 1)]), stay[:, halves[h]], ALU.mult)
+
+        own_term(0)
         nc.vector.tensor_tensor(pair[:], t[0][:], t[1][:], ALU.add)
-        nc.vector.tensor_tensor(res1[:], pair[:], t[2][:], ALU.add)
+        own_term(1)
+        for h in range(2):
+            nc.vector.tensor_tensor(res1[:, halves[h]], pair[:, halves[h]], own[h][:], ALU.add)
         nc.sync.dma_start(out[P : 2 * P, :], res1[:])

@@ -26,13 +26,13 @@ def tile_picked_grand_none_p_kernel(tc, x_words, x_scales, w1, gate, offs, cen, 
         reused = ctx.enter_context(tc.tile_pool(name="reused", bufs=1))
         psum = ctx.enter_context(tc.psum_pool(name="psum", bufs=1))
 
-        at = {"table_scales": 0, "gate_cols": 2048}
+        at = {"table_scales": 0, "gate_rows": 2048, "w_raw0": 4096, "w_codes01": 8192}
         at["picked_words0"] = at["table_scales"]
-        for i, name in enumerate(("grouped00", "grouped10", "grouped01", "grouped11")):
-            at[name] = at["gate_cols"] + 1024 * i
-        at["picked_words1"] = at["grouped00"]
-        at["w_codes10"] = at["grouped01"]
-        at["w_codes01"] = at["gate_cols"] + 4096
+        at["grouped0"] = at["gate_rows"]
+        at["picked_words1"] = at["grouped0"]
+        at["gates"] = at["w_raw0"]
+        at["grouped01"] = at["w_raw0"] + 2048
+        at["grouped11"] = at["w_raw0"] + 3072
         at["stay"] = at["w_codes01"]
 
         def sbuf(name, shape, dtype):
@@ -52,13 +52,9 @@ def tile_picked_grand_none_p_kernel(tc, x_words, x_scales, w1, gate, offs, cen, 
         nc.gpsimd.memset(gate_rows[:], 0.0)
         ident = keep.tile([P, P], F32, name="ident")
         make_identity(nc, ident[:])
-        moved_scales = keep.tile([P, S], U8, name="moved_scales", align_bytes=64)
+        moved_scales = keep.tile([P, 2 * S], U8, name="moved_scales", align_bytes=64)
         nc.gpsimd.memset(moved_scales[:].bitcast(I32), 0)
-        w_raw0 = sbuf("w_raw0", [P, 4, N], F32)
-        w_raw1 = [sbuf("w_raw1%d" % b, [P, 4, P], F32) for b in range(2)]
-        w_raw = {(b, 0): w_raw0[:, :, P * b : P * (b + 1)] for b in range(2)}
-        for b in range(2):
-            w_raw[b, 1] = w_raw1[b][:]
+        w_raw = [sbuf("w_raw%d" % z, [P, 4, N], F32) for z in range(2)]
 
         def load_words(z):
             nc.sync.dma_start(table_words[z][:].bitcast(I32), x_words[z].bitcast(I32))
@@ -66,24 +62,20 @@ def tile_picked_grand_none_p_kernel(tc, x_words, x_scales, w1, gate, offs, cen, 
         w_rows = w1.rearrange("(z p j) m -> z p j m", z=2, j=4)
 
         offs_t = load_list("offs_t", offs)
-        nc.sync.dma_start(w_raw0[:, 0:2, :], w_rows[0][:, 0:2, :])
-        nc.sync.dma_start(gate_rows[0:4, :], gate[:, 0, :].rearrange("d (h v) -> h d v", h=2))
-        scale_rows = x_scales.bitcast(I32).rearrange("z (q r) c -> r q z c", r=4)
-        for r in range(4):
-            (nc.sync if r < 2 else nc.scalar).dma_start(table_scales[r:P:16, :].bitcast(I32), scale_rows[r])
         load_words(0)
-        nc.sync.dma_start(w_raw0[:, 2:4, :], w_rows[0][:, 2:4, :])
+        nc.sync.dma_start(table_scales[0:P:4, :].bitcast(I32), x_scales.bitcast(I32).rearrange("z s c -> s z c"))
+        nc.sync.dma_start(gate_rows[0:4, :], gate[:, 0, :].rearrange("d (h v) -> h d v", h=2))
         pos1_t = load_list("pos1_t", pos1)
         pos2_t = load_list("pos2_t", pos2)
         cen_t = load_list("cen_t", cen)
+        nc.sync.dma_start(w_raw[0][:], w_rows[0])
         load_words(1)
-        for b in range(2):
-            nc.sync.dma_start(w_raw1[b][:], w_rows[1][:, :, P * b : P * (b + 1)])
+        nc.sync.dma_start(w_raw[1][:], w_rows[1])
 
         gate_cols_ps = psum.tile([P, P], F32, name="gate_cols_ps", tag="t0")
         nc.tensor.transpose(gate_cols_ps[:], gate_rows[:], ident[:])
-        gate_cols = sbuf("gate_cols", [P, 1024], F32)
-        nc.scalar.copy(gate_cols[:, 0:4], gate_cols_ps[:, 0:4])
+        gate_cols = sbuf("gate_cols", [P, 4], F32)
+        nc.scalar.copy(gate_cols[:], gate_cols_ps[:, 0:4])
         spread = psum.tile([P, 2, 2, P], F32, name="spread", tag="t1")
         spread_sum = psum.tile([P, 2, P], F32, name="spread_sum", tag="t0")
         for d in range(2):
@@ -96,39 +88,38 @@ def tile_picked_grand_none_p_kernel(tc, x_words, x_scales, w1, gate, offs, cen, 
                     start=(d == 0 and h == 0), stop=(d == 1 and h == 1), is_transpose=True,
                 )
 
-        gates = sbuf("gates", [P, 2, V], F32)
-        nc.scalar.copy(gates[:].rearrange("p d v -> p (d v)"), spread[:].rearrange("p d h v -> p (d h v)"))
 
         picked_scales = keep.tile([P, S], U8, name="picked_scales", align_bytes=64)
         nc.vector.tensor_copy(picked_scales[:], table_scales[:].indirect(offs_t[:]))
-        picked_words = [sbuf("picked_words0", [P, S], U16)]
-        nc.vector.tensor_copy(picked_words[0][:], table_words[0][:].indirect(offs_t[:]))
         for q in range(4):
-            nc.sync.dma_start(moved_scales[32 * q : 32 * q + 4, :].bitcast(I32), picked_scales[32 * q + 16 : 32 * q + 20, :].bitcast(I32))
-        x_planes = [picked_scales, moved_scales]
+            nc.sync.dma_start(moved_scales[32 * q : 32 * q + 4, :].bitcast(I32), picked_scales[32 * q : 32 * (q + 1) : 4, :].bitcast(I32))
+        x_planes = [moved_scales[:, S * z : S * (z + 1)] for z in range(2)]
 
-        def cast(b, z, copy):
-            grouped = sbuf("grouped%d%d" % (b, z), [P, P, 4], BF16)
-            copy(
+        def pick_words(z):
+            words = sbuf("picked_words%d" % z, [P, S], U16)
+            nc.vector.tensor_copy(words[:], table_words[z][:].indirect(offs_t[:]))
+            return words
+
+        def quantise(name, z, first, width):
+            grouped = sbuf("grouped" + name, [P, width, 4], BF16)
+            nc.scalar.copy(
                 grouped[:].rearrange("p (c i) t -> p c t i", i=4),
-                w_raw[b, z].rearrange("p t (c i) -> p c t i", i=4),
+                w_raw[z][:, :, first : first + width].rearrange("p t (c i) -> p c t i", i=4),
             )
-            return grouped
-
-        def quantise(b, z, grouped):
-            codes = sbuf("w_codes%d%d" % (b, z), [P, P], U32)
-            plane = keep.tile([P, P], U8, name="w_scales%d%d" % (b, z), align_bytes=64)
+            codes = sbuf("w_codes" + name, [P, width], U32)
+            plane = sbuf("w_scales" + name, [P, width], U8)
             nc.vector.quantize_mx(out=codes[:].bitcast(FP8X4), scales=plane[:], in_=grouped[:].rearrange("p c t -> p (c t)"))
             return codes, plane
 
-        weights = {}
-        weights[0, 0] = quantise(0, 0, cast(0, 0, nc.scalar.copy))
-        late = cast(1, 0, nc.scalar.copy)
-        picked_words.append(sbuf("picked_words1", [P, S], U16))
-        nc.vector.tensor_copy(picked_words[1][:], table_words[1][:].indirect(offs_t[:]))
-        weights[0, 1] = quantise(0, 1, cast(0, 1, nc.scalar.copy))
-        weights[1, 0] = quantise(1, 0, late)
-        weights[1, 1] = quantise(1, 1, cast(1, 1, nc.scalar.copy))
+        picked_words = [pick_words(0)]
+        codes, plane = quantise("0", 0, 0, N)
+        weights = {(b, 0): (codes[:, P * b : P * (b + 1)], plane[:, P * b : P * (b + 1)]) for b in range(2)}
+        gates = sbuf("gates", [P, 2, V], F32)
+        nc.scalar.copy(gates[:].rearrange("p d v -> p (d v)"), spread[:].rearrange("p d h v -> p (d h v)"))
+        picked_words.append(pick_words(1))
+        for b in range(2):
+            codes, plane = quantise("%d1" % b, 1, P * b, P)
+            weights[b, 1] = (codes[:], plane[:])
 
         y = [keep.tile([P, S], F32, name="y%d" % b) for b in range(2)]
         pieces = {
@@ -146,8 +137,8 @@ def tile_picked_grand_none_p_kernel(tc, x_words, x_scales, w1, gate, offs, cen, 
                     cols = slice(P * g, P * (g + 1))
                     nc.tensor.matmul_mx(
                         out=bank[:, i, :],
-                        lhsT=codes[:].bitcast(FP8X4),
-                        lhsT_scale=plane[:],
+                        lhsT=codes.bitcast(FP8X4),
+                        lhsT_scale=plane,
                         rhs=picked_words[z][:, cols].bitcast(FP4X4),
                         rhs_scale=x_planes[z][:, cols],
                         start=first and i == 0,
@@ -157,11 +148,11 @@ def tile_picked_grand_none_p_kernel(tc, x_words, x_scales, w1, gate, offs, cen, 
                     copy(y[b][:, P * piece[0] : P * (piece[-1] + 1)], bank[:].rearrange("p g c -> p (g c)"))
 
         project(0, 0, True)
+        project(1, 0, True)
         project(0, 1, False)
         stay = sbuf("stay", [P, V], F32)
         nc.scalar.activation(stay[:], spread_sum[:].rearrange("p h v -> p (h v)"), COPY, bias=1.0, scale=-1.0)
-        project(1, 1, True)
-        project(1, 0, False)
+        project(1, 1, False)
 
         terms = [(pos1_t, gates[:, 0, :]), (pos2_t, gates[:, 1, :]), (cen_t, stay[:])]
 

@@ -26,14 +26,12 @@ def tile_picked_grand_none_p_kernel(tc, x_words, x_scales, w1, gate, offs, cen, 
         reused = ctx.enter_context(tc.tile_pool(name="reused", bufs=1))
         psum = ctx.enter_context(tc.psum_pool(name="psum", bufs=1))
 
-        at = {"table_scales": 0, "gate_rows": 2048, "w_raw0": 4096, "w_codes01": 8192}
-        at["picked_words0"] = at["table_scales"]
-        at["grouped0"] = at["gate_rows"]
-        at["picked_words1"] = at["grouped0"]
-        at["gates"] = at["w_raw0"]
-        at["grouped01"] = at["w_raw0"] + 2048
-        at["grouped11"] = at["w_raw0"] + 3072
-        at["stay"] = at["w_codes01"]
+        at = {"gate_rows": 0, "gate_cols": 4096}
+        for i, name in enumerate(("picked_words0", "picked_words1", "grouped10", "w_codes00")):
+            at[name] = at["gate_rows"] + 1024 * i
+        for b in range(2):
+            at["grouped%d1" % b] = at["gate_cols"] + 1024 * b
+        at["w_codes10"] = at["grouped01"]
 
         def sbuf(name, shape, dtype):
             if name in at:
@@ -48,34 +46,37 @@ def tile_picked_grand_none_p_kernel(tc, x_words, x_scales, w1, gate, offs, cen, 
         table_words = [sbuf("table_words%d" % z, [P, T], U16) for z in range(2)]
         table_scales = sbuf("table_scales", [P, T], U8)
         nc.vector.memset(table_scales[:].bitcast(I32), 0)
-        gate_rows = sbuf("gate_rows", [P, P], F32)
-        nc.gpsimd.memset(gate_rows[:], 0.0)
+        gate_rows = sbuf("gate_rows", [P, 1024], F32)
+        nc.gpsimd.memset(gate_rows[:, 0:P], 0.0)
         ident = keep.tile([P, P], F32, name="ident")
         make_identity(nc, ident[:])
         moved_scales = keep.tile([P, 2 * S], U8, name="moved_scales", align_bytes=64)
         nc.gpsimd.memset(moved_scales[:].bitcast(I32), 0)
-        w_raw = [sbuf("w_raw%d" % z, [P, 4, N], F32) for z in range(2)]
 
         def load_words(z):
             nc.sync.dma_start(table_words[z][:].bitcast(I32), x_words[z].bitcast(I32))
 
         w_rows = w1.rearrange("(z p j) m -> z p j m", z=2, j=4)
+        w_raw0 = sbuf("w_raw0", [P, 4, N], F32)
+        w_raw = {(b, 0): w_raw0[:, :, P * b : P * (b + 1)] for b in range(2)}
 
+        nc.sync.dma_start(w_raw0[:], w_rows[0])
         offs_t = load_list("offs_t", offs)
-        load_words(0)
+        nc.sync.dma_start(gate_rows[0:4, 0:P], gate[:, 0, :].rearrange("d (h v) -> h d v", h=2))
         nc.sync.dma_start(table_scales[0:P:4, :].bitcast(I32), x_scales.bitcast(I32).rearrange("z s c -> s z c"))
-        nc.sync.dma_start(gate_rows[0:4, :], gate[:, 0, :].rearrange("d (h v) -> h d v", h=2))
         pos1_t = load_list("pos1_t", pos1)
+        load_words(0)
         pos2_t = load_list("pos2_t", pos2)
-        cen_t = load_list("cen_t", cen)
-        nc.sync.dma_start(w_raw[0][:], w_rows[0])
         load_words(1)
-        nc.sync.dma_start(w_raw[1][:], w_rows[1])
+        cen_t = load_list("cen_t", cen)
+        for b in range(2):
+            w_raw[b, 1] = sbuf("w_raw%d1" % b, [P, 4, P], F32)[:]
+            nc.sync.dma_start(w_raw[b, 1], w_rows[1][:, :, P * b : P * (b + 1)])
 
         gate_cols_ps = psum.tile([P, P], F32, name="gate_cols_ps", tag="t0")
-        nc.tensor.transpose(gate_cols_ps[:], gate_rows[:], ident[:])
-        gate_cols = sbuf("gate_cols", [P, 4], F32)
-        nc.scalar.copy(gate_cols[:], gate_cols_ps[:, 0:4])
+        nc.tensor.transpose(gate_cols_ps[:], gate_rows[:, 0:P], ident[:])
+        gate_cols = sbuf("gate_cols", [P, 512], F32)
+        nc.scalar.copy(gate_cols[:, 0:4], gate_cols_ps[:, 0:4])
         spread = psum.tile([P, 2, 2, P], F32, name="spread", tag="t1")
         spread_sum = psum.tile([P, 2, P], F32, name="spread_sum", tag="t0")
         for d in range(2):
@@ -100,34 +101,35 @@ def tile_picked_grand_none_p_kernel(tc, x_words, x_scales, w1, gate, offs, cen, 
             nc.vector.tensor_copy(words[:], table_words[z][:].indirect(offs_t[:]))
             return words
 
-        def quantise(name, z, first, width):
-            grouped = sbuf("grouped" + name, [P, width, 4], BF16)
-            nc.scalar.copy(
-                grouped[:].rearrange("p (c i) t -> p c t i", i=4),
-                w_raw[z][:, :, first : first + width].rearrange("p t (c i) -> p c t i", i=4),
-            )
-            codes = sbuf("w_codes" + name, [P, width], U32)
-            plane = sbuf("w_scales" + name, [P, width], U8)
+        def cast(b, z):
+            grouped = sbuf("grouped%d%d" % (b, z), [P, P, 4], BF16)
+            nc.scalar.copy(grouped[:].rearrange("p (c i) t -> p c t i", i=4), w_raw[b, z].rearrange("p t (c i) -> p c t i", i=4))
+            return grouped
+
+        def quantise(b, z, grouped):
+            codes = sbuf("w_codes%d%d" % (b, z), [P, P], U32)
+            plane = sbuf("w_scales%d%d" % (b, z), [P, P], U8)
             nc.vector.quantize_mx(out=codes[:].bitcast(FP8X4), scales=plane[:], in_=grouped[:].rearrange("p c t -> p (c t)"))
-            return codes, plane
+            return codes[:], plane[:]
 
         picked_words = [pick_words(0)]
-        codes, plane = quantise("0", 0, 0, N)
-        weights = {(b, 0): (codes[:, P * b : P * (b + 1)], plane[:, P * b : P * (b + 1)]) for b in range(2)}
-        gates = sbuf("gates", [P, 2, V], F32)
-        nc.scalar.copy(gates[:].rearrange("p d v -> p (d v)"), spread[:].rearrange("p d h v -> p (d h v)"))
+        weights = {(0, 0): quantise(0, 0, cast(0, 0))}
         picked_words.append(pick_words(1))
-        for b in range(2):
-            codes, plane = quantise("%d1" % b, 1, P * b, P)
-            weights[b, 1] = (codes[:], plane[:])
+        grouped10 = cast(1, 0)
+        factors = sbuf("factors", [P, 3, V], F32)
+        nc.scalar.copy(factors[:, 0:2, :].rearrange("p d v -> p (d v)"), spread[:].rearrange("p d h v -> p (d h v)"))
+        nc.scalar.activation(factors[:, 2, :], spread_sum[:].rearrange("p h v -> p (h v)"), COPY, bias=1.0, scale=-1.0)
+        weights[0, 1] = quantise(0, 1, cast(0, 1))
+        weights[1, 0] = quantise(1, 0, grouped10)
+        weights[1, 1] = quantise(1, 1, cast(1, 1))
 
         y = [keep.tile([P, S], F32, name="y%d" % b) for b in range(2)]
         pieces = {
-            0: [((0,), nc.scalar.copy), ((1,), nc.vector.tensor_copy), ((2,), nc.scalar.copy), ((3,), nc.vector.tensor_copy)],
+            0: [((0,), nc.vector.tensor_copy), ((1,), nc.scalar.copy), ((2,), nc.vector.tensor_copy), ((3,), nc.scalar.copy)],
             1: [((0, 1), nc.scalar.copy), ((2, 3), nc.scalar.copy)],
         }
         banks = {
-            b: [psum.tile([P, len(piece), P], F32, name="bank%d%d" % (b, i)) for i, (piece, copy) in enumerate(pieces[b])] for b in range(2)
+            b: [psum.tile([P, len(piece), P], F32, name="bank%d%d" % (b, i), tag="bank%d%d" % (b, i)) for i, (piece, copy) in enumerate(pieces[b])] for b in range(2)
         }
 
         def project(b, z, first):
@@ -148,35 +150,30 @@ def tile_picked_grand_none_p_kernel(tc, x_words, x_scales, w1, gate, offs, cen, 
                     copy(y[b][:, P * piece[0] : P * (piece[-1] + 1)], bank[:].rearrange("p g c -> p (g c)"))
 
         project(0, 0, True)
-        project(1, 0, True)
         project(0, 1, False)
-        stay = sbuf("stay", [P, V], F32)
-        nc.scalar.activation(stay[:], spread_sum[:].rearrange("p h v -> p (h v)"), COPY, bias=1.0, scale=-1.0)
+        project(1, 0, True)
         project(1, 1, False)
 
-        terms = [(pos1_t, gates[:, 0, :]), (pos2_t, gates[:, 1, :]), (cen_t, stay[:])]
+        terms = [(places, factors[:, d, :]) for d, places in enumerate((pos1_t, pos2_t, cen_t))]
 
         def weighted(b, d):
             places, factor = terms[d]
-            term = keep.tile([P, V], F32, name="term%d%d" % (b, d))
+            term = sbuf("term%d%d" % (b, d), [P, V], F32)
             nc.vector.tensor_tensor(term[:], y[b][:].indirect(places[:]), factor, ALU.mult)
             return term
 
-        turned = psum.tile([P, 2, P], F32, name="turned", tag="t0")
+        turned = [psum.tile([P, P], F32, name="turned%d" % h, tag="bank0%d" % h) for h in range(2)]
         for d in range(3):
             term = weighted(0, d)
             for h in range(2):
-                nc.tensor.matmul(
-                    turned[:, h, :], term[:, P * h : P * (h + 1)], ident[:],
-                    start=(d == 0 and h == 0), stop=(d == 2 and h == 1), is_transpose=True,
-                )
-        turned_sum = keep.tile([P, 2, P], F32, name="turned_sum")
-        nc.scalar.copy(turned_sum[:], turned[:])
-        back = psum.tile([P, 2, P], F32, name="back", tag="t1")
-        for h in range(2):
-            nc.tensor.transpose(back[:, h, :], turned_sum[:, h, :], ident[:])
+                nc.tensor.matmul(turned[h][:], term[:, P * h : P * (h + 1)], ident[:], start=(d == 0), stop=(d == 2), is_transpose=True)
         res0 = keep.tile([P, V], F32, name="res0")
-        nc.scalar.copy(res0[:], back[:].rearrange("p h v -> p (h v)"))
+        for h in range(2):
+            turned_sum = keep.tile([P, P], F32, name="turned_sum%d" % h)
+            nc.scalar.copy(turned_sum[:], turned[h][:])
+            back = psum.tile([P, P], F32, name="back%d" % h, tag="bank0%d" % (2 + h))
+            nc.tensor.transpose(back[:], turned_sum[:], ident[:])
+            nc.scalar.copy(res0[:, P * h : P * (h + 1)], back[:])
         nc.sync.dma_start(out[0:P, :], res0[:])
 
         t = [weighted(1, d) for d in range(2)]
@@ -186,7 +183,7 @@ def tile_picked_grand_none_p_kernel(tc, x_words, x_scales, w1, gate, offs, cen, 
         own = [keep.tile([P, V // 2], F32, name="own%d" % h) for h in range(2)]
 
         def own_term(h):
-            nc.vector.tensor_tensor(own[h][:], y[1][:].indirect(cen_t[:, 8 * h : 8 * (h + 1)]), stay[:, halves[h]], ALU.mult)
+            nc.vector.tensor_tensor(own[h][:], y[1][:].indirect(cen_t[:, 8 * h : 8 * (h + 1)]), factors[:, 2, halves[h]], ALU.mult)
 
         own_term(0)
         nc.vector.tensor_tensor(pair[:], t[0][:], t[1][:], ALU.add)

@@ -66,12 +66,13 @@ def tile_picked_grand_none_p_kernel(tc, x_words, x_scales, w1, gate, offs, cen, 
         nc.sync.dma_start(table_scales[0:P:4, :].bitcast(I32), x_scales.bitcast(I32).rearrange("z s c -> s z c"))
         pos1_t = load_list("pos1_t", pos1)
         load_words(0)
-        pos2_t = load_list("pos2_t", pos2)
         load_words(1)
-        cen_t = load_list("cen_t", cen)
+        w_raw1 = sbuf("w_raw1", [P, 4, N], F32)
+        nc.sync.dma_start(w_raw1[:], w_rows[1])
         for b in range(2):
-            w_raw[b, 1] = sbuf("w_raw%d1" % b, [P, 4, P], F32)[:]
-            nc.sync.dma_start(w_raw[b, 1], w_rows[1][:, :, P * b : P * (b + 1)])
+            w_raw[b, 1] = w_raw1[:, :, P * b : P * (b + 1)]
+        pos2_t = load_list("pos2_t", pos2)
+        cen_t = load_list("cen_t", cen)
 
         gate_cols_ps = psum.tile([P, P], F32, name="gate_cols_ps", tag="t0")
         nc.tensor.transpose(gate_cols_ps[:], gate_rows[:, 0:P], ident[:])

@@ -29,9 +29,12 @@ def tile_picked_grand_none_p_kernel(tc, x_words, x_scales, w1, gate, offs, cen, 
         at = {"gate_rows": 0, "gate_cols": 4096}
         for i, name in enumerate(("picked_words0", "picked_words1", "grouped10", "w_codes00")):
             at[name] = at["gate_rows"] + 1024 * i
-        for b in range(2):
-            at["grouped%d1" % b] = at["gate_cols"] + 1024 * b
-        at["w_codes10"] = at["grouped01"]
+        at["grouped01b"] = at["w_codes00"] + 512
+        at["grouped01a"] = at["gate_cols"]
+        at["grouped11"] = at["gate_cols"] + 1024
+        at["w_codes10"] = at["grouped01a"]
+        at["w_codes01"] = at["gate_cols"] + 2048
+        at["stay"] = at["w_codes01"]
 
         def sbuf(name, shape, dtype):
             if name in at:
@@ -78,6 +81,8 @@ def tile_picked_grand_none_p_kernel(tc, x_words, x_scales, w1, gate, offs, cen, 
         nc.tensor.transpose(gate_cols_ps[:], gate_rows[:, 0:P], ident[:])
         gate_cols = sbuf("gate_cols", [P, 512], F32)
         nc.scalar.copy(gate_cols[:, 0:4], gate_cols_ps[:, 0:4])
+        sum_cols = sbuf("sum_cols", [P, 4], F32)
+        nc.scalar.copy(sum_cols[:], gate_cols_ps[:, 0:4])
         spread = psum.tile([P, 2, 2, P], F32, name="spread", tag="t1")
         spread_sum = psum.tile([P, 2, P], F32, name="spread_sum", tag="t0")
         for d in range(2):
@@ -86,7 +91,7 @@ def tile_picked_grand_none_p_kernel(tc, x_words, x_scales, w1, gate, offs, cen, 
         for d in range(2):
             for h in range(2):
                 nc.tensor.matmul(
-                    spread_sum[:, h, :], gate_cols[:, 2 * h + d : 2 * h + d + 1].to_broadcast([P, P]), ident[:],
+                    spread_sum[:, h, :], sum_cols[:, 2 * h + d : 2 * h + d + 1].to_broadcast([P, P]), ident[:],
                     start=(d == 0 and h == 0), stop=(d == 1 and h == 1), is_transpose=True,
                 )
 
@@ -102,27 +107,31 @@ def tile_picked_grand_none_p_kernel(tc, x_words, x_scales, w1, gate, offs, cen, 
             nc.vector.tensor_copy(words[:], table_words[z][:].indirect(offs_t[:]))
             return words
 
-        def cast(b, z):
-            grouped = sbuf("grouped%d%d" % (b, z), [P, P, 4], BF16)
-            nc.scalar.copy(grouped[:].rearrange("p (c i) t -> p c t i", i=4), w_raw[b, z].rearrange("p t (c i) -> p c t i", i=4))
+        def cast(name, raw, copy=nc.scalar.copy):
+            grouped = sbuf("grouped" + name, [P, raw.shape[2], 4], BF16)
+            copy(grouped[:].rearrange("p (c i) t -> p c t i", i=4), raw.rearrange("p t (c i) -> p c t i", i=4))
             return grouped
 
-        def quantise(b, z, grouped):
+        weights = {}
+
+        def quantise(b, z, *parts):
             codes = sbuf("w_codes%d%d" % (b, z), [P, P], U32)
             plane = sbuf("w_scales%d%d" % (b, z), [P, P], U8)
-            nc.vector.quantize_mx(out=codes[:].bitcast(FP8X4), scales=plane[:], in_=grouped[:].rearrange("p c t -> p (c t)"))
-            return codes[:], plane[:]
+            width = P // len(parts)
+            for i, grouped in enumerate(parts):
+                cols = slice(width * i, width * (i + 1))
+                nc.vector.quantize_mx(out=codes[:, cols].bitcast(FP8X4), scales=plane[:, cols], in_=grouped[:].rearrange("p c t -> p (c t)"))
+            weights[b, z] = (codes[:], plane[:])
 
         picked_words = [pick_words(0)]
-        weights = {(0, 0): quantise(0, 0, cast(0, 0))}
+        quantise(0, 0, cast("00", w_raw[0, 0]))
         picked_words.append(pick_words(1))
-        grouped10 = cast(1, 0)
-        factors = sbuf("factors", [P, 3, V], F32)
-        nc.scalar.copy(factors[:, 0:2, :].rearrange("p d v -> p (d v)"), spread[:].rearrange("p d h v -> p (d h v)"))
-        nc.scalar.activation(factors[:, 2, :], spread_sum[:].rearrange("p h v -> p (h v)"), COPY, bias=1.0, scale=-1.0)
-        weights[0, 1] = quantise(0, 1, cast(0, 1))
-        weights[1, 0] = quantise(1, 0, grouped10)
-        weights[1, 1] = quantise(1, 1, cast(1, 1))
+        grouped10 = cast("10", w_raw[1, 0])
+        gates = sbuf("gates", [P, 2, V], F32)
+        nc.scalar.copy(gates[:].rearrange("p d v -> p (d v)"), spread[:].rearrange("p d h v -> p (d h v)"))
+        quantise(0, 1, cast("01a", w_raw[0, 1][:, :, 0 : P // 2]), cast("01b", w_raw[0, 1][:, :, P // 2 : P], nc.vector.tensor_copy))
+        quantise(1, 0, grouped10)
+        quantise(1, 1, cast("11", w_raw[1, 1]))
 
         y = [keep.tile([P, S], F32, name="y%d" % b) for b in range(2)]
         pieces = {
@@ -152,10 +161,12 @@ def tile_picked_grand_none_p_kernel(tc, x_words, x_scales, w1, gate, offs, cen, 
 
         project(0, 0, True)
         project(0, 1, False)
+        stay = sbuf("stay", [P, V], F32)
+        nc.scalar.activation(stay[:], spread_sum[:].rearrange("p h v -> p (h v)"), COPY, bias=1.0, scale=-1.0)
         project(1, 0, True)
         project(1, 1, False)
 
-        terms = [(places, factors[:, d, :]) for d, places in enumerate((pos1_t, pos2_t, cen_t))]
+        terms = [(pos1_t, gates[:, 0, :]), (pos2_t, gates[:, 1, :]), (cen_t, stay[:])]
 
         def weighted(b, d):
             places, factor = terms[d]
@@ -184,7 +195,7 @@ def tile_picked_grand_none_p_kernel(tc, x_words, x_scales, w1, gate, offs, cen, 
         own = [keep.tile([P, V // 2], F32, name="own%d" % h) for h in range(2)]
 
         def own_term(h):
-            nc.vector.tensor_tensor(own[h][:], y[1][:].indirect(cen_t[:, 8 * h : 8 * (h + 1)]), factors[:, 2, halves[h]], ALU.mult)
+            nc.vector.tensor_tensor(own[h][:], y[1][:].indirect(cen_t[:, 8 * h : 8 * (h + 1)]), stay[:, halves[h]], ALU.mult)
 
         own_term(0)
         nc.vector.tensor_tensor(pair[:], t[0][:], t[1][:], ALU.add)

@@ -50,11 +50,12 @@ def tile_picked_grand_none_p_kernel(tc, x_words, x_scales, w1, gate, offs, cen, 
         table_scales = sbuf("table_scales", [P, T], U8)
         nc.vector.memset(table_scales[:].bitcast(I32), 0)
         gate_rows = sbuf("gate_rows", [P, 1024], F32)
-        nc.gpsimd.memset(gate_rows[:, 0:P], 0.0)
+        nc.vector.memset(gate_rows[:, 0:P], 0.0)
         ident = keep.tile([P, P], F32, name="ident")
-        make_identity(nc, ident[:])
+        nc.vector.memset(ident[:], 0.0)
+        make_identity(nc, ident[:], nomemset=True)
         moved_scales = keep.tile([P, 2 * S], U8, name="moved_scales", align_bytes=64)
-        nc.gpsimd.memset(moved_scales[:].bitcast(I32), 0)
+        nc.vector.memset(moved_scales[:].bitcast(I32), 0)
 
         def load_words(z):
             nc.sync.dma_start(table_words[z][:].bitcast(I32), x_words[z].bitcast(I32))
@@ -65,8 +66,8 @@ def tile_picked_grand_none_p_kernel(tc, x_words, x_scales, w1, gate, offs, cen, 
 
         nc.sync.dma_start(w_raw0[:], w_rows[0])
         offs_t = load_list("offs_t", offs)
-        nc.sync.dma_start(gate_rows[0:4, 0:P], gate[:, 0, :].rearrange("d (h v) -> h d v", h=2))
         nc.sync.dma_start(table_scales[0:P:4, :].bitcast(I32), x_scales.bitcast(I32).rearrange("z s c -> s z c"))
+        nc.sync.dma_start(gate_rows[0:4, 0:P], gate[:, 0, :].rearrange("d (h v) -> h d v", h=2))
         pos1_t = load_list("pos1_t", pos1)
         load_words(0)
         load_words(1)

@@ -27,9 +27,9 @@ def tile_picked_grand_none_p_kernel(tc, x_words, x_scales, w1, gate, offs, cen, 
         psum = ctx.enter_context(tc.psum_pool(name="psum", bufs=1))
 
         at = {"gate_rows": 0, "gate_cols": 4096}
-        for i, name in enumerate(("picked_words0", "picked_words1", "grouped10", "w_codes00")):
-            at[name] = at["gate_rows"] + 1024 * i
-        at["grouped01b"] = at["w_codes00"] + 512
+        at["w_raw0"] = 8192
+        for i, name in enumerate(("picked_words0", "picked_words1", "grouped01b")):
+            at[name] = at["w_raw0"] + 1024 * i
         at["grouped01a"] = at["gate_cols"]
         at["grouped11"] = at["gate_cols"] + 1024
         at["w_codes10"] = at["grouped01a"]
@@ -49,7 +49,7 @@ def tile_picked_grand_none_p_kernel(tc, x_words, x_scales, w1, gate, offs, cen, 
         table_words = [sbuf("table_words%d" % z, [P, T], U16) for z in range(2)]
         table_scales = sbuf("table_scales", [P, T], U8)
         nc.vector.memset(table_scales[:].bitcast(I32), 0)
-        gate_rows = sbuf("gate_rows", [P, 1024], F32)
+        gate_rows = sbuf("gate_rows", [P, P], F32)
         nc.vector.memset(gate_rows[:, 0:P], 0.0)
         ident = keep.tile([P, P], F32, name="ident")
         nc.vector.memset(ident[:], 0.0)
@@ -68,15 +68,34 @@ def tile_picked_grand_none_p_kernel(tc, x_words, x_scales, w1, gate, offs, cen, 
         offs_t = load_list("offs_t", offs)
         nc.sync.dma_start(table_scales[0:P:4, :].bitcast(I32), x_scales.bitcast(I32).rearrange("z s c -> s z c"))
         nc.sync.dma_start(gate_rows[0:4, 0:P], gate[:, 0, :].rearrange("d (h v) -> h d v", h=2))
-        pos1_t = load_list("pos1_t", pos1)
         load_words(0)
         load_words(1)
         w_raw1 = sbuf("w_raw1", [P, 4, N], F32)
         nc.sync.dma_start(w_raw1[:], w_rows[1])
         for b in range(2):
             w_raw[b, 1] = w_raw1[:, :, P * b : P * (b + 1)]
+        pos1_t = load_list("pos1_t", pos1)
         pos2_t = load_list("pos2_t", pos2)
         cen_t = load_list("cen_t", cen)
+
+        def cast(name, raw, copy=nc.scalar.copy):
+            grouped = sbuf("grouped" + name, [P, raw.shape[2], 4], BF16)
+            copy(grouped[:].rearrange("p (c i) t -> p c t i", i=4), raw.rearrange("p t (c i) -> p c t i", i=4))
+            return grouped
+
+        weights = {}
+
+        def quantise(b, z, *parts):
+            codes = sbuf("w_codes%d%d" % (b, z), [P, P], U32)
+            plane = sbuf("w_scales%d%d" % (b, z), [P, P], U8)
+            width = P // len(parts)
+            for i, grouped in enumerate(parts):
+                cols = slice(width * i, width * (i + 1))
+                nc.vector.quantize_mx(out=codes[:, cols].bitcast(FP8X4), scales=plane[:, cols], in_=grouped[:].rearrange("p c t -> p (c t)"))
+            weights[b, z] = (codes[:], plane[:])
+
+        grouped00 = cast("00", w_raw[0, 0])
+        grouped10 = cast("10", w_raw[1, 0])
 
         gate_cols_ps = psum.tile([P, P], F32, name="gate_cols_ps", tag="t0")
         nc.tensor.transpose(gate_cols_ps[:], gate_rows[:, 0:P], ident[:])
@@ -108,26 +127,8 @@ def tile_picked_grand_none_p_kernel(tc, x_words, x_scales, w1, gate, offs, cen, 
             nc.vector.tensor_copy(words[:], table_words[z][:].indirect(offs_t[:]))
             return words
 
-        def cast(name, raw, copy=nc.scalar.copy):
-            grouped = sbuf("grouped" + name, [P, raw.shape[2], 4], BF16)
-            copy(grouped[:].rearrange("p (c i) t -> p c t i", i=4), raw.rearrange("p t (c i) -> p c t i", i=4))
-            return grouped
-
-        weights = {}
-
-        def quantise(b, z, *parts):
-            codes = sbuf("w_codes%d%d" % (b, z), [P, P], U32)
-            plane = sbuf("w_scales%d%d" % (b, z), [P, P], U8)
-            width = P // len(parts)
-            for i, grouped in enumerate(parts):
-                cols = slice(width * i, width * (i + 1))
-                nc.vector.quantize_mx(out=codes[:, cols].bitcast(FP8X4), scales=plane[:, cols], in_=grouped[:].rearrange("p c t -> p (c t)"))
-            weights[b, z] = (codes[:], plane[:])
-
-        picked_words = [pick_words(0)]
-        quantise(0, 0, cast("00", w_raw[0, 0]))
-        picked_words.append(pick_words(1))
-        grouped10 = cast("10", w_raw[1, 0])
+        quantise(0, 0, grouped00)
+        picked_words = [pick_words(z) for z in range(2)]
         gates = sbuf("gates", [P, 2, V], F32)
         nc.scalar.copy(gates[:].rearrange("p d v -> p (d v)"), spread[:].rearrange("p d h v -> p (d h v)"))
         quantise(0, 1, cast("01a", w_raw[0, 1][:, :, 0 : P // 2]), cast("01b", w_raw[0, 1][:, :, P // 2 : P], nc.vector.tensor_copy))

@@ -32,6 +32,7 @@ def tile_picked_grand_none_p_kernel(tc, x_words, x_scales, w1, gate, offs, cen, 
             at[name] = at["w_raw0"] + 1024 * i
         at["grouped01a"] = at["gate_cols"]
         at["grouped11"] = at["gate_cols"] + 1024
+        at["sum_cols"] = at["grouped11"]
         at["w_codes10"] = at["grouped01a"]
         at["w_codes01"] = at["gate_cols"] + 2048
         at["stay"] = at["w_codes01"]
@@ -75,8 +76,6 @@ def tile_picked_grand_none_p_kernel(tc, x_words, x_scales, w1, gate, offs, cen, 
         for b in range(2):
             w_raw[b, 1] = w_raw1[:, :, P * b : P * (b + 1)]
         pos1_t = load_list("pos1_t", pos1)
-        pos2_t = load_list("pos2_t", pos2)
-        cen_t = load_list("cen_t", cen)
 
         def cast(name, raw, copy=nc.scalar.copy):
             grouped = sbuf("grouped" + name, [P, raw.shape[2], 4], BF16)
@@ -99,7 +98,7 @@ def tile_picked_grand_none_p_kernel(tc, x_words, x_scales, w1, gate, offs, cen, 
 
         gate_cols_ps = psum.tile([P, P], F32, name="gate_cols_ps", tag="t0")
         nc.tensor.transpose(gate_cols_ps[:], gate_rows[:, 0:P], ident[:])
-        gate_cols = sbuf("gate_cols", [P, 512], F32)
+        gate_cols = sbuf("gate_cols", [P, 4], F32)
         nc.scalar.copy(gate_cols[:, 0:4], gate_cols_ps[:, 0:4])
         sum_cols = sbuf("sum_cols", [P, 4], F32)
         nc.scalar.copy(sum_cols[:], gate_cols_ps[:, 0:4])
@@ -120,6 +119,8 @@ def tile_picked_grand_none_p_kernel(tc, x_words, x_scales, w1, gate, offs, cen, 
         nc.vector.tensor_copy(picked_scales[:], table_scales[:].indirect(offs_t[:]))
         for q in range(4):
             nc.sync.dma_start(moved_scales[32 * q : 32 * q + 4, :].bitcast(I32), picked_scales[32 * q : 32 * (q + 1) : 4, :].bitcast(I32))
+        pos2_t = load_list("pos2_t", pos2)
+        cen_t = load_list("cen_t", cen)
         x_planes = [moved_scales[:, S * z : S * (z + 1)] for z in range(2)]
 
         def pick_words(z):

@@ -102,6 +102,8 @@ def tile_picked_grand_none_p_kernel(tc, x_words, x_scales, w1, gate, offs, cen, 
         nc.scalar.copy(gate_cols[:, 0:4], gate_cols_ps[:, 0:4])
         sum_cols = sbuf("sum_cols", [P, 4], F32)
         nc.scalar.copy(sum_cols[:], gate_cols_ps[:, 0:4])
+        near_cols = sbuf("near_cols", [P, 4], F32)
+        nc.scalar.copy(near_cols[:], gate_cols_ps[:, 0:4])
         spread = psum.tile([P, 2, 2, P], F32, name="spread", tag="t1")
         spread_sum = psum.tile([P, 2, P], F32, name="spread_sum", tag="t0")
         for d in range(2):
@@ -169,40 +171,49 @@ def tile_picked_grand_none_p_kernel(tc, x_words, x_scales, w1, gate, offs, cen, 
         project(1, 0, True)
         project(1, 1, False)
 
-        terms = [(pos1_t, gates[:, 0, :]), (pos2_t, gates[:, 1, :]), (cen_t, stay[:])]
+        halves = [slice(0, V // 2), slice(V // 2, V)]
 
-        def weighted(b, d):
-            places, factor = terms[d]
-            term = sbuf("term%d%d" % (b, d), [P, V], F32)
+        def weighted(name, b, places, factor):
+            term = keep.tile([P, V], F32, name=name)
             nc.vector.tensor_tensor(term[:], y[b][:].indirect(places[:]), factor, ALU.mult)
             return term
 
+        def fetched(name, b, places):
+            term = keep.tile([P, V], F32, name=name)
+            nc.scalar.activation(term[:], y[b][:].indirect(places[:]), COPY)
+            return term
+
+        near0 = fetched("near0", 0, pos1_t)
         turned = [psum.tile([P, P], F32, name="turned%d" % h, tag="bank0%d" % h) for h in range(2)]
-        for d in range(3):
-            term = weighted(0, d)
+        for d, (places, factor) in enumerate(((pos2_t, gates[:, 1, :]), (cen_t, stay[:]))):
+            term = weighted("term0%d" % d, 0, places, factor)
             for h in range(2):
-                nc.tensor.matmul(turned[h][:], term[:, P * h : P * (h + 1)], ident[:], start=(d == 0), stop=(d == 2), is_transpose=True)
-        res0 = keep.tile([P, V], F32, name="res0")
+                nc.tensor.matmul(turned[h][:], term[:, halves[h]], ident[:], start=(d == 0), stop=(d == 1), is_transpose=True)
+        near1 = fetched("near1", 1, pos1_t)
+        near_turned = psum.tile([P, 2, P], F32, name="near_turned", tag="bank11")
         for h in range(2):
+            nc.tensor.transpose(near_turned[:, h, :], near0[:, halves[h]], ident[:])
+        res0 = keep.tile([P, V], F32, name="res0")
+        back = [psum.tile([P, P], F32, name="back%d" % h, tag="bank0%d" % (2 + h)) for h in range(2)]
+        for h in range(2):
+            near_scaled = keep.tile([P, P], F32, name="near_scaled%d" % h)
+            nc.scalar.activation(near_scaled[:], near_turned[:, h, :], COPY, scale=near_cols[:, 2 * h : 2 * h + 1])
             turned_sum = keep.tile([P, P], F32, name="turned_sum%d" % h)
             nc.scalar.copy(turned_sum[:], turned[h][:])
-            back = psum.tile([P, P], F32, name="back%d" % h, tag="bank0%d" % (2 + h))
-            nc.tensor.transpose(back[:], turned_sum[:], ident[:])
-            nc.scalar.copy(res0[:, P * h : P * (h + 1)], back[:])
+            nc.tensor.matmul(back[h][:], near_scaled[:], ident[:], start=True, stop=False, is_transpose=True)
+            nc.tensor.matmul(back[h][:], turned_sum[:], ident[:], start=False, stop=True, is_transpose=True)
+        for h in range(2):
+            nc.scalar.copy(res0[:, halves[h]], back[h][:])
         nc.sync.dma_start(out[0:P, :], res0[:])
 
-        t = [weighted(1, d) for d in range(2)]
+        far1 = weighted("far1", 1, pos2_t, gates[:, 1, :])
+        own1 = weighted("own1", 1, cen_t, stay[:])
+        near1_scaled = keep.tile([P, V], F32, name="near1_scaled")
+        nc.vector.tensor_tensor(near1_scaled[:], near1[:], gates[:, 0, :], ALU.mult)
         pair = keep.tile([P, V], F32, name="pair")
         res1 = keep.tile([P, V], F32, name="res1")
-        halves = [slice(0, V // 2), slice(V // 2, V)]
-        own = [keep.tile([P, V // 2], F32, name="own%d" % h) for h in range(2)]
-
-        def own_term(h):
-            nc.vector.tensor_tensor(own[h][:], y[1][:].indirect(cen_t[:, 8 * h : 8 * (h + 1)]), stay[:, halves[h]], ALU.mult)
-
-        own_term(0)
-        nc.vector.tensor_tensor(pair[:], t[0][:], t[1][:], ALU.add)
-        own_term(1)
         for h in range(2):
-            nc.vector.tensor_tensor(res1[:, halves[h]], pair[:, halves[h]], own[h][:], ALU.add)
+            nc.vector.tensor_tensor(pair[:, halves[h]], far1[:, halves[h]], own1[:, halves[h]], ALU.add)
+        for h in range(2):
+            nc.vector.tensor_tensor(res1[:, halves[h]], pair[:, halves[h]], near1_scaled[:, halves[h]], ALU.add)
         nc.sync.dma_start(out[P : 2 * P, :], res1[:])

@@ -26,16 +26,15 @@ def tile_picked_grand_none_p_kernel(tc, x_words, x_scales, w1, gate, offs, cen, 
         reused = ctx.enter_context(tc.tile_pool(name="reused", bufs=1))
         psum = ctx.enter_context(tc.psum_pool(name="psum", bufs=1))
 
-        at = {"gate_rows": 0, "gate_cols": 4096}
+        at = {"gate_rows": 0, "gate_cols0": 4096}
         at["w_raw0"] = 8192
         for i, name in enumerate(("picked_words0", "picked_words1", "grouped01b")):
             at[name] = at["w_raw0"] + 1024 * i
-        at["grouped01a"] = at["gate_cols"]
-        at["grouped11"] = at["gate_cols"] + 1024
-        at["sum_cols"] = at["grouped11"]
+        at["grouped01a"] = at["gate_cols0"]
+        at["grouped11"] = at["gate_cols0"] + 1024
+        at["gate_cols1"] = at["grouped11"]
         at["w_codes10"] = at["grouped01a"]
-        at["w_codes01"] = at["gate_cols"] + 2048
-        at["stay"] = at["w_codes01"]
+        at["w_codes01"] = at["w_codes11"] = at["gate_cols0"] + 2048
 
         def sbuf(name, shape, dtype):
             if name in at:
@@ -98,24 +97,23 @@ def tile_picked_grand_none_p_kernel(tc, x_words, x_scales, w1, gate, offs, cen, 
 
         gate_cols_ps = psum.tile([P, P], F32, name="gate_cols_ps", tag="t0")
         nc.tensor.transpose(gate_cols_ps[:], gate_rows[:, 0:P], ident[:])
-        gate_cols = sbuf("gate_cols", [P, 4], F32)
-        nc.scalar.copy(gate_cols[:, 0:4], gate_cols_ps[:, 0:4])
-        sum_cols = sbuf("sum_cols", [P, 4], F32)
-        nc.scalar.copy(sum_cols[:], gate_cols_ps[:, 0:4])
+        gate_cols = [sbuf("gate_cols%d" % h, [P, 2], F32) for h in range(2)]
+        sum_cols = sbuf("sum_cols", [P, 2], F32)
+        for h in range(2):
+            nc.scalar.activation(gate_cols[h][:], gate_cols_ps[:, 2 * h : 2 * h + 2], COPY, accum_out=sum_cols[:, h : h + 1])
         near_cols = sbuf("near_cols", [P, 4], F32)
         nc.scalar.copy(near_cols[:], gate_cols_ps[:, 0:4])
-        spread = psum.tile([P, 2, 2, P], F32, name="spread", tag="t1")
         spread_sum = psum.tile([P, 2, P], F32, name="spread_sum", tag="t0")
+        for h in range(2):
+            nc.tensor.transpose(spread_sum[:, h, :], sum_cols[:, h : h + 1].to_broadcast([P, P]), ident[:])
+        stay = sbuf("stay", [P, V], F32)
+        nc.scalar.activation(stay[:], spread_sum[:].rearrange("p h v -> p (h v)"), COPY, bias=1.0, scale=-1.0)
+        gates = sbuf("gates", [P, 2, V], F32)
         for d in range(2):
+            spread = psum.tile([P, 2, P], F32, name="spread%d" % d, tag=("t1", "bank11")[d])
             for h in range(2):
-                nc.tensor.transpose(spread[:, d, h, :], gate_cols[:, 2 * h + d : 2 * h + d + 1].to_broadcast([P, P]), ident[:])
-        for d in range(2):
-            for h in range(2):
-                nc.tensor.matmul(
-                    spread_sum[:, h, :], sum_cols[:, 2 * h + d : 2 * h + d + 1].to_broadcast([P, P]), ident[:],
-                    start=(d == 0 and h == 0), stop=(d == 1 and h == 1), is_transpose=True,
-                )
-
+                nc.tensor.transpose(spread[:, h, :], gate_cols[h][:, d : d + 1].to_broadcast([P, P]), ident[:])
+            nc.scalar.copy(gates[:, d, :], spread[:].rearrange("p h v -> p (h v)"))
 
         picked_scales = keep.tile([P, S], U8, name="picked_scales", align_bytes=64)
         nc.vector.tensor_copy(picked_scales[:], table_scales[:].indirect(offs_t[:]))
@@ -132,15 +130,13 @@ def tile_picked_grand_none_p_kernel(tc, x_words, x_scales, w1, gate, offs, cen, 
 
         quantise(0, 0, grouped00)
         picked_words = [pick_words(z) for z in range(2)]
-        gates = sbuf("gates", [P, 2, V], F32)
-        nc.scalar.copy(gates[:].rearrange("p d v -> p (d v)"), spread[:].rearrange("p d h v -> p (d h v)"))
         quantise(0, 1, cast("01a", w_raw[0, 1][:, :, 0 : P // 2]), cast("01b", w_raw[0, 1][:, :, P // 2 : P], nc.vector.tensor_copy))
         quantise(1, 0, grouped10)
-        quantise(1, 1, cast("11", w_raw[1, 1]))
+        grouped11 = cast("11", w_raw[1, 1])
 
         y = [keep.tile([P, S], F32, name="y%d" % b) for b in range(2)]
         pieces = {
-            0: [((0,), nc.vector.tensor_copy), ((1,), nc.scalar.copy), ((2,), nc.vector.tensor_copy), ((3,), nc.scalar.copy)],
+            0: [((0,), nc.vector.tensor_copy), ((1,), nc.vector.tensor_copy), ((2,), nc.vector.tensor_copy), ((3,), nc.scalar.copy)],
             1: [((0, 1), nc.scalar.copy), ((2, 3), nc.scalar.copy)],
         }
         banks = {
@@ -166,8 +162,7 @@ def tile_picked_grand_none_p_kernel(tc, x_words, x_scales, w1, gate, offs, cen, 
 
         project(0, 0, True)
         project(0, 1, False)
-        stay = sbuf("stay", [P, V], F32)
-        nc.scalar.activation(stay[:], spread_sum[:].rearrange("p h v -> p (h v)"), COPY, bias=1.0, scale=-1.0)
+        quantise(1, 1, grouped11)
         project(1, 0, True)
         project(1, 1, False)
 
@@ -184,23 +179,24 @@ def tile_picked_grand_none_p_kernel(tc, x_words, x_scales, w1, gate, offs, cen, 
             return term
 
         near0 = fetched("near0", 0, pos1_t)
+        near_turned = psum.tile([P, 2, P], F32, name="near_turned", tag="t1")
+        for h in range(2):
+            nc.tensor.transpose(near_turned[:, h, :], near0[:, halves[h]], ident[:])
+        near_scaled = [keep.tile([P, P], F32, name="near_scaled%d" % h) for h in range(2)]
+        for h in range(2):
+            nc.scalar.activation(near_scaled[h][:], near_turned[:, h, :], COPY, scale=near_cols[:, 2 * h : 2 * h + 1])
+        near1 = fetched("near1", 1, pos1_t)
         turned = [psum.tile([P, P], F32, name="turned%d" % h, tag="bank0%d" % h) for h in range(2)]
         for d, (places, factor) in enumerate(((pos2_t, gates[:, 1, :]), (cen_t, stay[:]))):
             term = weighted("term0%d" % d, 0, places, factor)
             for h in range(2):
                 nc.tensor.matmul(turned[h][:], term[:, halves[h]], ident[:], start=(d == 0), stop=(d == 1), is_transpose=True)
-        near1 = fetched("near1", 1, pos1_t)
-        near_turned = psum.tile([P, 2, P], F32, name="near_turned", tag="bank11")
-        for h in range(2):
-            nc.tensor.transpose(near_turned[:, h, :], near0[:, halves[h]], ident[:])
         res0 = keep.tile([P, V], F32, name="res0")
         back = [psum.tile([P, P], F32, name="back%d" % h, tag="bank0%d" % (2 + h)) for h in range(2)]
         for h in range(2):
-            near_scaled = keep.tile([P, P], F32, name="near_scaled%d" % h)
-            nc.scalar.activation(near_scaled[:], near_turned[:, h, :], COPY, scale=near_cols[:, 2 * h : 2 * h + 1])
             turned_sum = keep.tile([P, P], F32, name="turned_sum%d" % h)
             nc.scalar.copy(turned_sum[:], turned[h][:])
-            nc.tensor.matmul(back[h][:], near_scaled[:], ident[:], start=True, stop=False, is_transpose=True)
+            nc.tensor.matmul(back[h][:], near_scaled[h][:], ident[:], start=True, stop=False, is_transpose=True)
             nc.tensor.matmul(back[h][:], turned_sum[:], ident[:], start=False, stop=True, is_transpose=True)
         for h in range(2):
             nc.scalar.copy(res0[:, halves[h]], back[h][:])

@@ -17,6 +17,7 @@ FP8X4 = mybir.dt.float8_e4m3fn_x4
 FP4X4 = mybir.dt.float4_e2m1fn_x4
 ALU = mybir.AluOpType
 COPY = mybir.ActivationFunctionType.Copy
+KIB = 1024
 
 
 def tile_picked_grand_none_p_kernel(tc, x_words, x_scales, w1, gate, offs, cen, pos1, pos2, out):
@@ -26,15 +27,13 @@ def tile_picked_grand_none_p_kernel(tc, x_words, x_scales, w1, gate, offs, cen, 
         reused = ctx.enter_context(tc.tile_pool(name="reused", bufs=1))
         psum = ctx.enter_context(tc.psum_pool(name="psum", bufs=1))
 
-        at = {"gate_rows": 0, "gate_cols0": 4096}
-        at["w_raw0"] = 8192
+        at = {"gate_rows": 0, "gate_cols0": 4 * KIB, "w_raw0": 8 * KIB}
         for i, name in enumerate(("picked_words0", "picked_words1", "grouped01b")):
-            at[name] = at["w_raw0"] + 1024 * i
+            at[name] = at["w_raw0"] + KIB * i
         at["grouped01a"] = at["gate_cols0"]
-        at["grouped11"] = at["gate_cols0"] + 1024
-        at["gate_cols1"] = at["grouped11"]
+        at["grouped11"] = at["gate_cols1"] = at["gate_cols0"] + KIB
         at["w_codes10"] = at["grouped01a"]
-        at["w_codes01"] = at["w_codes11"] = at["gate_cols0"] + 2048
+        at["w_codes01"] = at["w_codes11"] = at["gate_cols0"] + 2 * KIB
 
         def sbuf(name, shape, dtype):
             if name in at:
@@ -50,30 +49,29 @@ def tile_picked_grand_none_p_kernel(tc, x_words, x_scales, w1, gate, offs, cen, 
         table_scales = sbuf("table_scales", [P, T], U8)
         nc.vector.memset(table_scales[:].bitcast(I32), 0)
         gate_rows = sbuf("gate_rows", [P, P], F32)
-        nc.vector.memset(gate_rows[:, 0:P], 0.0)
+        nc.vector.memset(gate_rows[:], 0.0)
         ident = keep.tile([P, P], F32, name="ident")
         nc.vector.memset(ident[:], 0.0)
         make_identity(nc, ident[:], nomemset=True)
         moved_scales = keep.tile([P, 2 * S], U8, name="moved_scales", align_bytes=64)
         nc.vector.memset(moved_scales[:].bitcast(I32), 0)
 
-        def load_words(z):
-            nc.sync.dma_start(table_words[z][:].bitcast(I32), x_words[z].bitcast(I32))
+        w_rows = w1.rearrange("(z p t) m -> z p t m", z=2, t=4)
+        w_raw = {}
 
-        w_rows = w1.rearrange("(z p j) m -> z p j m", z=2, j=4)
-        w_raw0 = sbuf("w_raw0", [P, 4, N], F32)
-        w_raw = {(b, 0): w_raw0[:, :, P * b : P * (b + 1)] for b in range(2)}
+        def load_weights(z):
+            raw = sbuf("w_raw%d" % z, [P, 4, N], F32)
+            nc.sync.dma_start(raw[:], w_rows[z])
+            for b in range(2):
+                w_raw[b, z] = raw[:, :, P * b : P * (b + 1)]
 
-        nc.sync.dma_start(w_raw0[:], w_rows[0])
+        load_weights(0)
         offs_t = load_list("offs_t", offs)
         nc.sync.dma_start(table_scales[0:P:4, :].bitcast(I32), x_scales.bitcast(I32).rearrange("z s c -> s z c"))
-        nc.sync.dma_start(gate_rows[0:4, 0:P], gate[:, 0, :].rearrange("d (h v) -> h d v", h=2))
-        load_words(0)
-        load_words(1)
-        w_raw1 = sbuf("w_raw1", [P, 4, N], F32)
-        nc.sync.dma_start(w_raw1[:], w_rows[1])
-        for b in range(2):
-            w_raw[b, 1] = w_raw1[:, :, P * b : P * (b + 1)]
+        nc.sync.dma_start(gate_rows[0:4, :], gate[:, 0, :].rearrange("d (h v) -> h d v", h=2))
+        for z in range(2):
+            nc.sync.dma_start(table_words[z][:].bitcast(I32), x_words[z].bitcast(I32))
+        load_weights(1)
         pos1_t = load_list("pos1_t", pos1)
 
         def cast(name, raw, copy=nc.scalar.copy):
@@ -86,9 +84,9 @@ def tile_picked_grand_none_p_kernel(tc, x_words, x_scales, w1, gate, offs, cen, 
         def quantise(b, z, *parts):
             codes = sbuf("w_codes%d%d" % (b, z), [P, P], U32)
             plane = sbuf("w_scales%d%d" % (b, z), [P, P], U8)
-            width = P // len(parts)
+            part_cols = P // len(parts)
             for i, grouped in enumerate(parts):
-                cols = slice(width * i, width * (i + 1))
+                cols = slice(part_cols * i, part_cols * (i + 1))
                 nc.vector.quantize_mx(out=codes[:, cols].bitcast(FP8X4), scales=plane[:, cols], in_=grouped[:].rearrange("p c t -> p (c t)"))
             weights[b, z] = (codes[:], plane[:])
 
@@ -96,21 +94,21 @@ def tile_picked_grand_none_p_kernel(tc, x_words, x_scales, w1, gate, offs, cen, 
         grouped10 = cast("10", w_raw[1, 0])
 
         gate_cols_ps = psum.tile([P, P], F32, name="gate_cols_ps", tag="t0")
-        nc.tensor.transpose(gate_cols_ps[:], gate_rows[:, 0:P], ident[:])
+        nc.tensor.transpose(gate_cols_ps[:], gate_rows[:], ident[:])
         gate_cols = [sbuf("gate_cols%d" % h, [P, 2], F32) for h in range(2)]
         sum_cols = sbuf("sum_cols", [P, 2], F32)
         for h in range(2):
             nc.scalar.activation(gate_cols[h][:], gate_cols_ps[:, 2 * h : 2 * h + 2], COPY, accum_out=sum_cols[:, h : h + 1])
-        near_cols = sbuf("near_cols", [P, 4], F32)
-        nc.scalar.copy(near_cols[:], gate_cols_ps[:, 0:4])
+        near_cols = sbuf("near_cols", [P, 2], F32)
+        nc.scalar.copy(near_cols[:], gate_cols_ps[:, 0:4:2])
         spread_sum = psum.tile([P, 2, P], F32, name="spread_sum", tag="t0")
         for h in range(2):
             nc.tensor.transpose(spread_sum[:, h, :], sum_cols[:, h : h + 1].to_broadcast([P, P]), ident[:])
         stay = sbuf("stay", [P, V], F32)
         nc.scalar.activation(stay[:], spread_sum[:].rearrange("p h v -> p (h v)"), COPY, bias=1.0, scale=-1.0)
         gates = sbuf("gates", [P, 2, V], F32)
-        for d in range(2):
-            spread = psum.tile([P, 2, P], F32, name="spread%d" % d, tag=("t1", "bank11")[d])
+        for d, bank_tag in enumerate(("t1", "bank11")):
+            spread = psum.tile([P, 2, P], F32, name="spread%d" % d, tag=bank_tag)
             for h in range(2):
                 nc.tensor.transpose(spread[:, h, :], gate_cols[h][:, d : d + 1].to_broadcast([P, P]), ident[:])
             nc.scalar.copy(gates[:, d, :], spread[:].rearrange("p h v -> p (h v)"))
@@ -135,36 +133,34 @@ def tile_picked_grand_none_p_kernel(tc, x_words, x_scales, w1, gate, offs, cen, 
         grouped11 = cast("11", w_raw[1, 1])
 
         y = [keep.tile([P, S], F32, name="y%d" % b) for b in range(2)]
-        pieces = {
-            0: [((0,), nc.vector.tensor_copy), ((1,), nc.vector.tensor_copy), ((2,), nc.vector.tensor_copy), ((3,), nc.scalar.copy)],
-            1: [((0, 1), nc.scalar.copy), ((2, 3), nc.scalar.copy)],
-        }
-        banks = {
-            b: [psum.tile([P, len(piece), P], F32, name="bank%d%d" % (b, i), tag="bank%d%d" % (b, i)) for i, (piece, copy) in enumerate(pieces[b])] for b in range(2)
-        }
+        copies = ((nc.vector.tensor_copy,) * 3 + (nc.scalar.copy,), (nc.scalar.copy,) * 2)
+        banks = [
+            [psum.tile([P, S // len(copies[b])], F32, name="bank%d%d" % (b, i), tag="bank%d%d" % (b, i)) for i in range(len(copies[b]))]
+            for b in range(2)
+        ]
 
-        def project(b, z, first):
+        def project(b, z):
             codes, plane = weights[b, z]
-            for bank, (piece, copy) in zip(banks[b], pieces[b]):
-                for i, g in enumerate(piece):
-                    cols = slice(P * g, P * (g + 1))
-                    nc.tensor.matmul_mx(
-                        out=bank[:, i, :],
-                        lhsT=codes.bitcast(FP8X4),
-                        lhsT_scale=plane,
-                        rhs=picked_words[z][:, cols].bitcast(FP4X4),
-                        rhs_scale=x_planes[z][:, cols],
-                        start=first and i == 0,
-                        stop=not first and i == len(piece) - 1,
-                    )
-                if not first:
-                    copy(y[b][:, P * piece[0] : P * (piece[-1] + 1)], bank[:].rearrange("p g c -> p (g c)"))
+            bank_cols = S // len(copies[b])
+            for i, (bank, copy) in enumerate(zip(banks[b], copies[b])):
+                cols = slice(bank_cols * i, bank_cols * (i + 1))
+                nc.tensor.matmul_mx(
+                    out=bank[:],
+                    lhsT=codes.bitcast(FP8X4),
+                    lhsT_scale=plane,
+                    rhs=picked_words[z][:, cols].bitcast(FP4X4),
+                    rhs_scale=x_planes[z][:, cols],
+                    start=(z == 0),
+                    stop=(z == 1),
+                )
+                if z == 1:
+                    copy(y[b][:, cols], bank[:])
 
-        project(0, 0, True)
-        project(0, 1, False)
+        project(0, 0)
+        project(0, 1)
         quantise(1, 1, grouped11)
-        project(1, 0, True)
-        project(1, 1, False)
+        project(1, 0)
+        project(1, 1)
 
         halves = [slice(0, V // 2), slice(V // 2, V)]
 
@@ -184,7 +180,7 @@ def tile_picked_grand_none_p_kernel(tc, x_words, x_scales, w1, gate, offs, cen, 
             nc.tensor.transpose(near_turned[:, h, :], near0[:, halves[h]], ident[:])
         near_scaled = [keep.tile([P, P], F32, name="near_scaled%d" % h) for h in range(2)]
         for h in range(2):
-            nc.scalar.activation(near_scaled[h][:], near_turned[:, h, :], COPY, scale=near_cols[:, 2 * h : 2 * h + 1])
+            nc.scalar.activation(near_scaled[h][:], near_turned[:, h, :], COPY, scale=near_cols[:, h : h + 1])
         near1 = fetched("near1", 1, pos1_t)
         turned = [psum.tile([P, P], F32, name="turned%d" % h, tag="bank0%d" % h) for h in range(2)]
         for d, (places, factor) in enumerate(((pos2_t, gates[:, 1, :]), (cen_t, stay[:]))):

@@ -37,8 +37,8 @@ def tile_picked_grand_none_p_kernel(tc, x_words, x_scales, w1, gate, offs, cen, 
 
         def sbuf(name, shape, dtype):
             if name in at:
-                return reused.tile(shape, dtype, name=name, offset=at[name], align_bytes=64)
-            return keep.tile(shape, dtype, name=name, align_bytes=64)
+                return reused.tile(shape, dtype, name=name, offset=at[name], align_bytes=256)
+            return keep.tile(shape, dtype, name=name, align_bytes=256)
 
         def load_list(name, src):
             tile = keep.tile([P, src.shape[1]], U16, name=name)
@@ -53,7 +53,7 @@ def tile_picked_grand_none_p_kernel(tc, x_words, x_scales, w1, gate, offs, cen, 
         ident = keep.tile([P, P], F32, name="ident")
         nc.vector.memset(ident[:], 0.0)
         make_identity(nc, ident[:], nomemset=True)
-        moved_scales = keep.tile([P, 2 * S], U8, name="moved_scales", align_bytes=64)
+        moved_scales = keep.tile([P, 2 * S], U8, name="moved_scales", align_bytes=256)
         nc.vector.memset(moved_scales[:].bitcast(I32), 0)
 
         w_rows = w1.rearrange("(z p t) m -> z p t m", z=2, t=4)
@@ -113,7 +113,7 @@ def tile_picked_grand_none_p_kernel(tc, x_words, x_scales, w1, gate, offs, cen, 
                 nc.tensor.transpose(spread[:, h, :], gate_cols[h][:, d : d + 1].to_broadcast([P, P]), ident[:])
             nc.scalar.copy(gates[:, d, :], spread[:].rearrange("p h v -> p (h v)"))
 
-        picked_scales = keep.tile([P, S], U8, name="picked_scales", align_bytes=64)
+        picked_scales = keep.tile([P, S], U8, name="picked_scales", align_bytes=256)
         nc.vector.tensor_copy(picked_scales[:], table_scales[:].indirect(offs_t[:]))
         for q in range(4):
             nc.sync.dma_start(moved_scales[32 * q : 32 * q + 4, :].bitcast(I32), picked_scales[32 * q : 32 * (q + 1) : 4, :].bitcast(I32))

from contextlib import ExitStack

import concourse.mybir as mybir
from concourse.masks import make_identity

K, T, S, V, N = 1024, 2048, 512, 256, 256
P = 128
FLOPS = 2 * K * N * S

F32 = mybir.dt.float32
BF16 = mybir.dt.bfloat16
I32 = mybir.dt.int32
U16 = mybir.dt.uint16
U32 = mybir.dt.uint32
U8 = mybir.dt.uint8
FP8X4 = mybir.dt.float8_e4m3fn_x4
FP4X4 = mybir.dt.float4_e2m1fn_x4
ALU = mybir.AluOpType
COPY = mybir.ActivationFunctionType.Copy
KIB = 1024


def tile_picked_grand_none_p_kernel(tc, x_words, x_scales, w1, gate, offs, cen, pos1, pos2, out):
    nc = tc.nc
    with ExitStack() as ctx:
        keep = ctx.enter_context(tc.tile_pool(name="keep", bufs=1))
        reused = ctx.enter_context(tc.tile_pool(name="reused", bufs=1))
        psum = ctx.enter_context(tc.psum_pool(name="psum", bufs=1))

        at = {"gate_rows": 0, "gate_cols0": 4 * KIB, "w_raw0": 8 * KIB}
        for i, name in enumerate(("picked_words0", "picked_words1", "grouped01b")):
            at[name] = at["w_raw0"] + KIB * i
        at["grouped01a"] = at["gate_cols0"]
        at["grouped11"] = at["gate_cols1"] = at["gate_cols0"] + KIB
        at["w_codes10"] = at["grouped01a"]
        at["w_codes01"] = at["w_codes11"] = at["gate_cols0"] + 2 * KIB

        def sbuf(name, shape, dtype):
            if name in at:
                return reused.tile(shape, dtype, name=name, offset=at[name], align_bytes=256)
            return keep.tile(shape, dtype, name=name, align_bytes=256)

        def load_list(name, src):
            tile = keep.tile([P, src.shape[1]], U16, name=name)
            nc.sync.dma_start(tile[:], src)
            return tile

        table_words = [sbuf("table_words%d" % z, [P, T], U16) for z in range(2)]
        table_scales = sbuf("table_scales", [P, T], U8)
        nc.vector.memset(table_scales[:].bitcast(I32), 0)
        gate_rows = sbuf("gate_rows", [P, P], F32)
        nc.vector.memset(gate_rows[:], 0.0)
        ident = keep.tile([P, P], F32, name="ident")
        nc.vector.memset(ident[:], 0.0)
        make_identity(nc, ident[:], nomemset=True)
        moved_scales = keep.tile([P, 2 * S], U8, name="moved_scales", align_bytes=256)
        nc.vector.memset(moved_scales[:].bitcast(I32), 0)

        w_rows = w1.rearrange("(z p t) m -> z p t m", z=2, t=4)
        w_raw = {}

        def load_weights(z):
            raw = sbuf("w_raw%d" % z, [P, 4, N], F32)
            nc.sync.dma_start(raw[:], w_rows[z])
            for b in range(2):
                w_raw[b, z] = raw[:, :, P * b : P * (b + 1)]

        load_weights(0)
        offs_t = load_list("offs_t", offs)
        nc.sync.dma_start(table_scales[0:P:4, :].bitcast(I32), x_scales.bitcast(I32).rearrange("z s c -> s z c"))
        nc.sync.dma_start(gate_rows[0:4, :], gate[:, 0, :].rearrange("d (h v) -> h d v", h=2))
        for z in range(2):
            nc.sync.dma_start(table_words[z][:].bitcast(I32), x_words[z].bitcast(I32))
        load_weights(1)
        pos1_t = load_list("pos1_t", pos1)

        def cast(name, raw, copy=nc.scalar.copy):
            grouped = sbuf("grouped" + name, [P, raw.shape[2], 4], BF16)
            copy(grouped[:].rearrange("p (c i) t -> p c t i", i=4), raw.rearrange("p t (c i) -> p c t i", i=4))
            return grouped

        weights = {}

        def quantise(b, z, *parts):
            codes = sbuf("w_codes%d%d" % (b, z), [P, P], U32)
            plane = sbuf("w_scales%d%d" % (b, z), [P, P], U8)
            part_cols = P // len(parts)
            for i, grouped in enumerate(parts):
                cols = slice(part_cols * i, part_cols * (i + 1))
                nc.vector.quantize_mx(out=codes[:, cols].bitcast(FP8X4), scales=plane[:, cols], in_=grouped[:].rearrange("p c t -> p (c t)"))
            weights[b, z] = (codes[:], plane[:])

        grouped00 = cast("00", w_raw[0, 0])
        grouped10 = cast("10", w_raw[1, 0])

        gate_cols_ps = psum.tile([P, P], F32, name="gate_cols_ps", tag="t0")
        nc.tensor.transpose(gate_cols_ps[:], gate_rows[:], ident[:])
        gate_cols = [sbuf("gate_cols%d" % h, [P, 2], F32) for h in range(2)]
        sum_cols = sbuf("sum_cols", [P, 2], F32)
        for h in range(2):
            nc.scalar.activation(gate_cols[h][:], gate_cols_ps[:, 2 * h : 2 * h + 2], COPY, accum_out=sum_cols[:, h : h + 1])
        near_cols = sbuf("near_cols", [P, 2], F32)
        nc.scalar.copy(near_cols[:], gate_cols_ps[:, 0:4:2])
        spread_sum = psum.tile([P, 2, P], F32, name="spread_sum", tag="t0")
        for h in range(2):
            nc.tensor.transpose(spread_sum[:, h, :], sum_cols[:, h : h + 1].to_broadcast([P, P]), ident[:])
        stay = sbuf("stay", [P, V], F32)
        nc.scalar.activation(stay[:], spread_sum[:].rearrange("p h v -> p (h v)"), COPY, bias=1.0, scale=-1.0)
        gates = sbuf("gates", [P, 2, V], F32)
        for d, bank_tag in enumerate(("t1", "bank11")):
            spread = psum.tile([P, 2, P], F32, name="spread%d" % d, tag=bank_tag)
            for h in range(2):
                nc.tensor.transpose(spread[:, h, :], gate_cols[h][:, d : d + 1].to_broadcast([P, P]), ident[:])
            nc.scalar.copy(gates[:, d, :], spread[:].rearrange("p h v -> p (h v)"))

        picked_scales = keep.tile([P, S], U8, name="picked_scales", align_bytes=256)
        nc.vector.tensor_copy(picked_scales[:], table_scales[:].indirect(offs_t[:]))
        for q in range(4):
            nc.sync.dma_start(moved_scales[32 * q : 32 * q + 4, :].bitcast(I32), picked_scales[32 * q : 32 * (q + 1) : 4, :].bitcast(I32))
        pos2_t = load_list("pos2_t", pos2)
        cen_t = load_list("cen_t", cen)
        x_planes = [moved_scales[:, S * z : S * (z + 1)] for z in range(2)]

        def pick_words(z):
            words = sbuf("picked_words%d" % z, [P, S], U16)
            nc.vector.tensor_copy(words[:], table_words[z][:].indirect(offs_t[:]))
            return words

        quantise(0, 0, grouped00)
        picked_words = [pick_words(z) for z in range(2)]
        quantise(0, 1, cast("01a", w_raw[0, 1][:, :, 0 : P // 2]), cast("01b", w_raw[0, 1][:, :, P // 2 : P], nc.vector.tensor_copy))
        quantise(1, 0, grouped10)
        grouped11 = cast("11", w_raw[1, 1])

        y = [keep.tile([P, S], F32, name="y%d" % b) for b in range(2)]
        copies = ((nc.vector.tensor_copy,) * 3 + (nc.scalar.copy,), (nc.scalar.copy,) * 2)
        banks = [
            [psum.tile([P, S // len(copies[b])], F32, name="bank%d%d" % (b, i), tag="bank%d%d" % (b, i)) for i in range(len(copies[b]))]
            for b in range(2)
        ]

        def project(b, z):
            codes, plane = weights[b, z]
            bank_cols = S // len(copies[b])
            for i, (bank, copy) in enumerate(zip(banks[b], copies[b])):
                cols = slice(bank_cols * i, bank_cols * (i + 1))
                nc.tensor.matmul_mx(
                    out=bank[:],
                    lhsT=codes.bitcast(FP8X4),
                    lhsT_scale=plane,
                    rhs=picked_words[z][:, cols].bitcast(FP4X4),
                    rhs_scale=x_planes[z][:, cols],
                    start=(z == 0),
                    stop=(z == 1),
                )
                if z == 1:
                    copy(y[b][:, cols], bank[:])

        project(0, 0)
        project(0, 1)
        quantise(1, 1, grouped11)
        project(1, 0)
        project(1, 1)

        halves = [slice(0, V // 2), slice(V // 2, V)]

        def weighted(name, b, places, factor):
            term = keep.tile([P, V], F32, name=name)
            nc.vector.tensor_tensor(term[:], y[b][:].indirect(places[:]), factor, ALU.mult)
            return term

        def fetched(name, b, places):
            term = keep.tile([P, V], F32, name=name)
            nc.scalar.activation(term[:], y[b][:].indirect(places[:]), COPY)
            return term

        near0 = fetched("near0", 0, pos1_t)
        near_turned = psum.tile([P, 2, P], F32, name="near_turned", tag="t1")
        for h in range(2):
            nc.tensor.transpose(near_turned[:, h, :], near0[:, halves[h]], ident[:])
        near_scaled = [keep.tile([P, P], F32, name="near_scaled%d" % h) for h in range(2)]
        for h in range(2):
            nc.scalar.activation(near_scaled[h][:], near_turned[:, h, :], COPY, scale=near_cols[:, h : h + 1])
        near1 = fetched("near1", 1, pos1_t)
        turned = [psum.tile([P, P], F32, name="turned%d" % h, tag="bank0%d" % h) for h in range(2)]
        for d, (places, factor) in enumerate(((pos2_t, gates[:, 1, :]), (cen_t, stay[:]))):
            term = weighted("term0%d" % d, 0, places, factor)
            for h in range(2):
                nc.tensor.matmul(turned[h][:], term[:, halves[h]], ident[:], start=(d == 0), stop=(d == 1), is_transpose=True)
        res0 = keep.tile([P, V], F32, name="res0")
        back = [psum.tile([P, P], F32, name="back%d" % h, tag="bank0%d" % (2 + h)) for h in range(2)]
        for h in range(2):
            turned_sum = keep.tile([P, P], F32, name="turned_sum%d" % h)
            nc.scalar.copy(turned_sum[:], turned[h][:])
            nc.tensor.matmul(back[h][:], near_scaled[h][:], ident[:], start=True, stop=False, is_transpose=True)
            nc.tensor.matmul(back[h][:], turned_sum[:], ident[:], start=False, stop=True, is_transpose=True)
        for h in range(2):
            nc.scalar.copy(res0[:, halves[h]], back[h][:])
        nc.sync.dma_start(out[0:P, :], res0[:])

        far1 = weighted("far1", 1, pos2_t, gates[:, 1, :])
        own1 = weighted("own1", 1, cen_t, stay[:])
        near1_scaled = keep.tile([P, V], F32, name="near1_scaled")
        nc.vector.tensor_tensor(near1_scaled[:], near1[:], gates[:, 0, :], ALU.mult)
        pair = keep.tile([P, V], F32, name="pair")
        res1 = keep.tile([P, V], F32, name="res1")
        for h in range(2):
            nc.vector.tensor_tensor(pair[:, halves[h]], far1[:, halves[h]], own1[:, halves[h]], ALU.add)
        for h in range(2):
            nc.vector.tensor_tensor(res1[:, halves[h]], pair[:, halves[h]], near1_scaled[:, halves[h]], ALU.add)
        nc.sync.dma_start(out[P : 2 * P, :], res1[:])
